import numpy as np
import ml_dtypes


def mxq(x, axis, fmt="e4m3"):
    dtype, down = {"e4m3": (ml_dtypes.float8_e4m3fn, 7), "e5m2": (ml_dtypes.float8_e5m2, 14)}[fmt]
    v = np.moveaxis(np.asarray(x, np.float32).astype(ml_dtypes.bfloat16).astype(np.float64), axis, -1)
    blocks = v.reshape(v.shape[:-1] + (-1, 32))
    amax = np.abs(blocks).max(-1, keepdims=True)
    byte = np.maximum(np.where(amax > 0, np.frexp(amax)[1] - 1 + 127, 0) - down, 1)
    scale = np.exp2(byte - 127.0)
    codes = (blocks / scale).astype(np.float32).astype(dtype).astype(np.float64)
    return np.moveaxis((codes * scale).reshape(v.shape), -1, axis)


WIDE = False


def mx_kscale(k):
    if not WIDE:
        return np.ones(k)
    levels = np.array([10, -10, 5, -5, 0])
    if k % 512:
        return np.exp2(np.random.permutation(np.resize(levels, k // 32))).repeat(32)
    a = np.empty((k // 512, 16))
    for p in range(k // 512):
        a[p, :8] = np.random.permutation(np.resize(levels, 8))
        for g in range(8):
            far = levels[np.abs(levels - a[p, g]) >= 10]
            a[p, g + 8] = far[np.random.randint(len(far))]
    return np.exp2(a.ravel()).repeat(32)


def f64(x):
    return np.asarray(x).astype(np.float64)


def striped(idx):
    return np.tile(np.asarray(idx).reshape(-1, 16).T, (8, 1)).astype(np.uint16)


def unstriped(offs):
    return offs[:16].T.reshape(-1).astype(np.int64)


B, N, T, D, DV, NQ = 1, 512, 2048, 512, 512, 256


def setup_inputs():
    n = np.random.standard_normal
    idx = np.random.permutation(T)[:B * N]
    s = mx_kscale(D)[:, None]
    u = np.ones(T)
    u[idx] = mx_kscale(B * N)
    r = np.random.uniform(0.5, 2.0, T)
    rk = np.random.uniform(0.5, 2.0, T)
    k = n((D, T)) / s / rk
    v = n((DV, T)) / (u * r)
    return {
        "qT": (n((B, D, NQ)) * s * (0.60 / np.sqrt(D))).astype(np.float32),
        "kT": k.astype(np.float32),
        "vT": v.astype(np.float32),
        "ks": np.tile(rk, (128, 1)).astype(np.float32),
        "vs": np.tile(u * r, (128, 1)).astype(np.float32),
        "offs": striped(idx),
    }


def reference(qT, kT, vT, ks, vs, offs):
    idx = unstriped(offs)
    k = f64(kT)
    v = f64(vT)
    pick = lambda x: x[:, idx].reshape(x.shape[0], B, N).transpose(1, 0, 2)
    q = f64(qT)
    score = mxq(q, 1, "e4m3").transpose(0, 2, 1) @ mxq(pick(k), 1, "e4m3")
    score = score * pick(f64(ks))[:, :1, :]
    m = score.max(-1, keepdims=True)
    p = np.exp(score - m)
    total = p.sum(-1, keepdims=True)
    w = p * pick(f64(vs))[:, :1, :]
    y = mxq(w, 2, "e4m3") @ mxq(pick(v).transpose(0, 2, 1), 1, "e4m3")
    y = y / total
    return y

@@ -1,0 +1,193 @@
+from contextlib import ExitStack
+
+import concourse.mybir as mybir
+from concourse.masks import make_identity
+
+FLOPS = 2 * 2 * 256 * 512 * 512
+BYTES = 4 * (512 * 256 + 2 * 512 * 2048 + 2 * 2048 + 256 * 512) + 2 * 128 * 32
+
+F32 = mybir.dt.float32
+BF16 = mybir.dt.bfloat16
+U32 = mybir.dt.uint32
+U16 = mybir.dt.uint16
+U8 = mybir.dt.uint8
+FP8X4 = mybir.dt.float8_e4m3fn_x4
+MULT = mybir.AluOpType.mult
+MIN = mybir.AluOpType.min
+AXIS_X = mybir.AxisListType.X
+ACT = mybir.ActivationFunctionType
+
+P = 128
+PACK = 4
+T = 2048
+N = 512
+NQ = 256
+DV = 512
+QB = NQ // P
+EB = DV // P
+GATE = 8
+SB = N // P
+
+
+def tile_attend_mqa_topk_ks_kernel(tc, qT, kT, vT, ks, vs, offs, out):
+    nc = tc.nc
+    with ExitStack() as ctx:
+        keep = ctx.enter_context(tc.tile_pool(name="keep", bufs=1))
+        psum = ctx.enter_context(tc.psum_pool(name="psum", bufs=1))
+
+        offsets = keep.tile([P, N // 16], U16, name="offsets")
+        q_raw = keep.tile([P, PACK, NQ], F32, name="q_raw")
+        k_win = [keep.tile([P, T], F32, name=f"k_win{t}") for t in range(PACK)]
+        v_win = [keep.tile([P, T], F32, name=f"v_win{g}") for g in range(EB)]
+        ks_win = keep.tile([P, T], F32, name="ks_win")
+        vs_win = keep.tile([P, T], F32, name="vs_win")
+
+        k_planes = kT.rearrange("(p j) n -> j p n", j=PACK)
+        nc.sync.dma_start(offsets[:], offs)
+        nc.sync.dma_start(k_win[0][:], k_planes[0])
+        for win, row, split in ((vs_win, vs, 1024), (ks_win, ks, 1280)):
+            nc.vector.memset(win[:, 0:split], 0.0)
+            nc.gpsimd.memset(win[:, split:T], 0.0)
+            nc.scalar.dma_start(win[0:1, :], row[0:1, :])
+        nc.vector.memset(k_win[1][:, 0:GATE], 0.0)
+        nc.sync.dma_start(k_win[1][:], k_planes[1])
+        nc.vector.memset(q_raw[:, 0, 0:GATE], 0.0)
+        nc.sync.dma_start(q_raw[:], qT[0].rearrange("(p j) q -> p j q", j=PACK))
+        v_planes = vT.rearrange("(g e) n -> g e n", e=P)
+        pool_loads = [(k_win[2], k_planes[2]), (v_win[0], v_planes[0]), (k_win[3], k_planes[3])]
+        pool_loads += [(v_win[g], v_planes[g]) for g in range(1, EB)]
+        for win, plane in pool_loads:
+            nc.vector.memset(win[:, 0:GATE], 0.0)
+            nc.sync.dma_start(win[:], plane)
+
+        warm = keep.tile([P, 1], F32, name="warm")
+        nc.vector.memset(warm[:], 0.0)
+        nc.scalar.activation(warm[:], warm[:], ACT.Exp)
+
+        ident = keep.tile([P, P], F32, name="ident")
+        make_identity(nc, ident[:])
+
+        banks = [psum.tile([P, PACK, P], F32, name=f"bank{i}") for i in range(4)]
+
+        rows = keep.tile([P, 2, N], F32, name="rows")
+        ks_row, vs_row = rows[:, 0, :], rows[:, 1, :]
+        nks_col = keep.tile([P, SB], F32, name="nks_col")
+        vs_col = keep.tile([P, PACK], F32, name="vs_col")
+        nc.vector.tensor_copy(vs_row, vs_win[:].indirect(offsets[:]))
+        vs_t = banks[1]
+        for t in range(PACK):
+            nc.tensor.transpose(vs_t[:, t, :], vs_row[:, t::PACK], ident[:])
+        nc.vector.tensor_copy(vs_col[:], vs_t[:, :, 0])
+        nc.vector.tensor_copy(ks_row, ks_win[:].indirect(offsets[:]))
+        ks_t = banks[0]
+        for c in range(SB):
+            nc.tensor.transpose(ks_t[:, c, :], ks_row[:, c * P : (c + 1) * P], ident[:])
+        nc.vector.tensor_scalar(nks_col[:], ks_t[:, :, 0], -1.0, None, MULT)
+
+        q_bf = keep.tile([P, NQ, PACK], BF16, name="q_bf", align_bytes=64)
+        q_codes = keep.tile([P, NQ], U32, name="q_codes", align_bytes=64)
+        q_scales = keep.tile([P, NQ], U8, name="q_scales", align_bytes=64)
+        nc.scalar.copy(q_bf[:], q_raw[:].rearrange("p j q -> p q j"))
+        nc.vector.quantize_mx(q_codes[:].bitcast(FP8X4), q_scales[:], q_bf[:].rearrange("p q j -> p (q j)"))
+
+        k_bf = keep.tile([P, N, PACK], BF16, name="k_bf", align_bytes=64)
+        k_codes = keep.tile([P, N], U32, name="k_codes", align_bytes=64)
+        k_scales = keep.tile([P, N], U8, name="k_scales", align_bytes=64)
+        for t in range(PACK - 1):
+            nc.vector.tensor_copy(k_bf[:, :, t], k_win[t][:].indirect(offsets[:]))
+
+        v_bf = [keep.tile([P, 2 * P, PACK], BF16, name=f"v_bf{h}", align_bytes=64) for h in range(2)]
+        v_row0 = keep.tile([P, N], F32, name="v_row0")
+
+        def turn_values(g, row):
+            v_t = banks[(g + 2) % 4]
+            for t in range(PACK):
+                nc.tensor.transpose(v_t[:, t, :], row[:, t::PACK], ident[:])
+            e_cols = slice((g % 2) * P, (g % 2 + 1) * P)
+            nc.scalar.copy(v_bf[g // 2][:, e_cols, :], v_t[:].rearrange("s t e -> s e t"))
+
+        nc.vector.tensor_copy(v_row0[:], v_win[0][:].indirect(offsets[:]))
+        turn_values(0, v_row0)
+
+        nc.vector.tensor_copy(k_bf[:, :, PACK - 1], k_win[PACK - 1][:].indirect(offsets[:]))
+        half = N // 2
+        for h in range(2):
+            cols = slice(h * half, (h + 1) * half)
+            nc.vector.quantize_mx(
+                k_codes[:, cols].bitcast(FP8X4), k_scales[:, cols], k_bf[:, cols, :].rearrange("p n j -> p (n j)")
+            )
+
+        a_t = keep.tile([P, SB, NQ], F32, name="a_t")
+        for c in range(SB):
+            cols = slice(c * P, (c + 1) * P)
+            score = psum.tile([P, NQ], F32, name=f"score{c}", tag=f"sum{c}")
+            nc.tensor.matmul_mx(
+                score[:], k_codes[:, cols].bitcast(FP8X4), k_scales[:, cols], q_codes[:].bitcast(FP8X4), q_scales[:],
+                start=True, stop=True,
+            )
+            nc.scalar.activation(a_t[:, c, :], score[:], ACT.Copy, scale=nks_col[:, c : c + 1])
+
+        neg_m = keep.tile([P, QB], F32, name="neg_m")
+        total = [keep.tile([P, 1], F32, name=f"total{b}") for b in range(QB)]
+        inv = keep.tile([P, QB], F32, name="inv")
+        w_codes = keep.tile([P, NQ], U32, name="w_codes", align_bytes=64)
+        w_scales = keep.tile([P, NQ], U8, name="w_scales", align_bytes=64)
+        a_q = []
+        for b in range(QB):
+            a_b = banks[b]
+            for c in range(SB):
+                nc.tensor.transpose(a_b[:, c, :], a_t[:, c, b * P : (b + 1) * P], ident[:])
+            a_q.append(a_b)
+        p_sb = []
+        for b in range(QB):
+            nc.vector.tensor_reduce(neg_m[:, b : b + 1], a_q[b][:].rearrange("q c s -> q (c s)"), AXIS_X, MIN)
+            p_b = keep.tile([P, PACK, P], F32, name=f"p_sb{b}")
+            nc.scalar.activation(
+                p_b[:], a_q[b][:].rearrange("q c s -> q (c s)").rearrange("q (s t) -> q t s", t=PACK), ACT.Exp,
+                bias=neg_m[:, b : b + 1], scale=-1.0, accum_out=total[b][:],
+            )
+            p_sb.append(p_b)
+        for b in range(QB):
+            p_t = banks[b + 2]
+            for t in range(PACK):
+                nc.tensor.transpose(p_t[:, t, :], p_sb[b][:, t, :], ident[:])
+            w_bf = keep.tile([P, P, PACK], BF16, name=f"w_bf{b}", align_bytes=64)
+            nc.vector.tensor_tensor(
+                w_bf[:], p_t[:].rearrange("s t q -> s q t"),
+                vs_col[:].unsqueeze(1).to_broadcast([P, P, PACK]), MULT,
+            )
+            cols = slice(b * P, (b + 1) * P)
+            nc.vector.quantize_mx(
+                w_codes[:, cols].bitcast(FP8X4), w_scales[:, cols], w_bf[:].rearrange("s q t -> s (q t)")
+            )
+            nc.vector.reciprocal(inv[:, b : b + 1], total[b][:])
+
+        v_rows = [
+            v_row0[:],
+            a_t[:, 2:4, :].rearrange("s c q -> s (c q)"),
+            p_sb[1][:].rearrange("q t s -> q (t s)"),
+            p_sb[0][:].rearrange("q t s -> q (t s)"),
+        ]
+        for g in range(1, EB):
+            nc.vector.tensor_copy(v_rows[g], v_win[g][:].indirect(offsets[:]))
+        half_e = 2 * P
+        for h in range(2):
+            v_codes = keep.tile([P, half_e], U32, name=f"v_codes{h}", align_bytes=64)
+            v_scales = keep.tile([P, half_e], U8, name=f"v_scales{h}", align_bytes=64)
+            for g in (1,) if h == 0 else (2, 3):
+                turn_values(g, v_rows[g])
+            nc.vector.quantize_mx(v_codes[:].bitcast(FP8X4), v_scales[:], v_bf[h][:].rearrange("s e t -> s (e t)"))
+            for b in range(QB):
+                cols = slice(b * P, (b + 1) * P)
+                y = psum.tile([P, half_e], F32, name=f"y{h}_{b}", tag=f"sum{2 * h + b}")
+                nc.tensor.matmul_mx(
+                    y[:], w_codes[:, cols].bitcast(FP8X4), w_scales[:, cols], v_codes[:].bitcast(FP8X4), v_scales[:],
+                    start=True, stop=True,
+                )
+                y_sb = keep.tile([P, half_e], F32, name=f"y_sb{h}_{b}")
+                if h == 1 and b == 0:
+                    nc.vector.tensor_scalar(y_sb[:], y[:], inv[:, b : b + 1], None, MULT)
+                else:
+                    nc.scalar.activation(y_sb[:], y[:], ACT.Copy, scale=inv[:, b : b + 1])
+                queue = nc.scalar if h == 1 and b == 1 else nc.sync
+                queue.dma_start(out[0, cols, h * half_e : (h + 1) * half_e], y_sb[:])

@@ -14,6 +14,7 @@ U8 = mybir.dt.uint8
 FP8X4 = mybir.dt.float8_e4m3fn_x4
 MULT = mybir.AluOpType.mult
 MIN = mybir.AluOpType.min
+ADD = mybir.AluOpType.add
 AXIS_X = mybir.AxisListType.X
 ACT = mybir.ActivationFunctionType
 
@@ -25,7 +26,6 @@ NQ = 256
 DV = 512
 QB = NQ // P
 EB = DV // P
-GATE = 8
 SB = N // P
 
 
@@ -43,22 +43,18 @@ def tile_attend_mqa_topk_ks_kernel(tc, qT, kT, vT, ks, vs, offs, out):
         vs_win = keep.tile([P, T], F32, name="vs_win")
 
         k_planes = kT.rearrange("(p j) n -> j p n", j=PACK)
+        v_planes = vT.rearrange("(g e) n -> g e n", e=P)
         nc.sync.dma_start(offsets[:], offs)
-        nc.sync.dma_start(k_win[0][:], k_planes[0])
-        for win, row, split in ((vs_win, vs, 1024), (ks_win, ks, 1280)):
+        for t in range(PACK):
+            nc.sync.dma_start(k_win[t][:], k_planes[t])
+        nc.sync.dma_start(q_raw[:], qT[0].rearrange("(p j) q -> p j q", j=PACK))
+        for g in range(EB):
+            nc.sync.dma_start(v_win[g][:], v_planes[g])
+        split = 1280
+        for win, row in ((vs_win, vs), (ks_win, ks)):
             nc.vector.memset(win[:, 0:split], 0.0)
             nc.gpsimd.memset(win[:, split:T], 0.0)
             nc.scalar.dma_start(win[0:1, :], row[0:1, :])
-        nc.vector.memset(k_win[1][:, 0:GATE], 0.0)
-        nc.sync.dma_start(k_win[1][:], k_planes[1])
-        nc.vector.memset(q_raw[:, 0, 0:GATE], 0.0)
-        nc.sync.dma_start(q_raw[:], qT[0].rearrange("(p j) q -> p j q", j=PACK))
-        v_planes = vT.rearrange("(g e) n -> g e n", e=P)
-        pool_loads = [(k_win[2], k_planes[2]), (v_win[0], v_planes[0]), (k_win[3], k_planes[3])]
-        pool_loads += [(v_win[g], v_planes[g]) for g in range(1, EB)]
-        for win, plane in pool_loads:
-            nc.vector.memset(win[:, 0:GATE], 0.0)
-            nc.sync.dma_start(win[:], plane)
 
         warm = keep.tile([P, 1], F32, name="warm")
         nc.vector.memset(warm[:], 0.0)
@@ -67,127 +63,139 @@ def tile_attend_mqa_topk_ks_kernel(tc, qT, kT, vT, ks, vs, offs, out):
         ident = keep.tile([P, P], F32, name="ident")
         make_identity(nc, ident[:])
 
-        banks = [psum.tile([P, PACK, P], F32, name=f"bank{i}") for i in range(4)]
+        s_bank = [psum.tile([P, PACK, P], F32, name=f"s_bank{i}") for i in range(4)]
+        a_bank = [psum.tile([P, PACK, P], F32, name=f"a_bank{i}") for i in range(2)]
+        v_bank = [psum.tile([P, PACK, P], F32, name=f"v_bank{i}") for i in range(2)]
 
-        rows = keep.tile([P, 2, N], F32, name="rows")
-        ks_row, vs_row = rows[:, 0, :], rows[:, 1, :]
-        nks_col = keep.tile([P, SB], F32, name="nks_col")
-        vs_col = keep.tile([P, PACK], F32, name="vs_col")
-        nc.vector.tensor_copy(vs_row, vs_win[:].indirect(offsets[:]))
-        vs_t = banks[1]
-        for t in range(PACK):
-            nc.tensor.transpose(vs_t[:, t, :], vs_row[:, t::PACK], ident[:])
-        nc.vector.tensor_copy(vs_col[:], vs_t[:, :, 0])
-        nc.vector.tensor_copy(ks_row, ks_win[:].indirect(offsets[:]))
-        ks_t = banks[0]
-        for c in range(SB):
-            nc.tensor.transpose(ks_t[:, c, :], ks_row[:, c * P : (c + 1) * P], ident[:])
-        nc.vector.tensor_scalar(nks_col[:], ks_t[:, :, 0], -1.0, None, MULT)
-
-        q_bf = keep.tile([P, NQ, PACK], BF16, name="q_bf", align_bytes=64)
-        q_codes = keep.tile([P, NQ], U32, name="q_codes", align_bytes=64)
-        q_scales = keep.tile([P, NQ], U8, name="q_scales", align_bytes=64)
-        nc.scalar.copy(q_bf[:], q_raw[:].rearrange("p j q -> p q j"))
-        nc.vector.quantize_mx(q_codes[:].bitcast(FP8X4), q_scales[:], q_bf[:].rearrange("p q j -> p (q j)"))
+        def flat(bank, width):
+            return bank[:].rearrange("p c s -> p (c s)")[:, 0:width]
 
         k_bf = keep.tile([P, N, PACK], BF16, name="k_bf", align_bytes=64)
         k_codes = keep.tile([P, N], U32, name="k_codes", align_bytes=64)
         k_scales = keep.tile([P, N], U8, name="k_scales", align_bytes=64)
-        for t in range(PACK - 1):
+        k_pair = keep.tile([P, 2, N], F32, name="k_pair")
+        vs_row = keep.tile([P, N], F32, name="vs_row")
+        vs_dealt = keep.tile([P, PACK, P], F32, name="vs_dealt")
+        ks_row = keep.tile([P, N], F32, name="ks_row")
+        nks_col = keep.tile([P, SB], F32, name="nks_col")
+        vs_col = keep.tile([P, PACK], F32, name="vs_col")
+
+        nc.vector.tensor_copy(k_pair[:, 0, :], k_win[0][:].indirect(offsets[:]))
+        nc.vector.tensor_copy(vs_row[:], vs_win[:].indirect(offsets[:]))
+        nc.vector.tensor_copy(k_pair[:, 1, :], k_win[1][:].indirect(offsets[:]))
+        nc.vector.tensor_copy(ks_row[:], ks_win[:].indirect(offsets[:]))
+        nc.scalar.copy(
+            vs_dealt[:].rearrange("p (u e) (b r) -> p u e b r", u=2, r=8),
+            vs_row[:].rearrange("p (b u r e) -> p u e b r", u=2, r=8, e=2),
+        )
+        for t in range(PACK):
+            nc.tensor.transpose(a_bank[1][:, t, :], vs_dealt[:, t, :], ident[:])
+        nc.scalar.copy(vs_col[:], a_bank[1][:, :, 0])
+        nc.scalar.copy(k_bf[:, :, 0:2], k_pair[:].rearrange("p j n -> p n j"))
+        for c in range(SB):
+            nc.tensor.transpose(a_bank[0][:, c, :], ks_row[:, c * P : (c + 1) * P], ident[:])
+        nc.scalar.activation(nks_col[:], a_bank[0][:, :, 0], ACT.Copy, scale=-1.0)
+        for t in (2, 3):
             nc.vector.tensor_copy(k_bf[:, :, t], k_win[t][:].indirect(offsets[:]))
+        nc.vector.quantize_mx(k_codes[:].bitcast(FP8X4), k_scales[:], k_bf[:].rearrange("p n j -> p (n j)"))
 
-        v_bf = [keep.tile([P, 2 * P, PACK], BF16, name=f"v_bf{h}", align_bytes=64) for h in range(2)]
-        v_row0 = keep.tile([P, N], F32, name="v_row0")
-
-        def turn_values(g, row):
-            v_t = banks[(g + 2) % 4]
-            for t in range(PACK):
-                nc.tensor.transpose(v_t[:, t, :], row[:, t::PACK], ident[:])
-            e_cols = slice((g % 2) * P, (g % 2 + 1) * P)
-            nc.scalar.copy(v_bf[g // 2][:, e_cols, :], v_t[:].rearrange("s t e -> s e t"))
-
-        nc.vector.tensor_copy(v_row0[:], v_win[0][:].indirect(offsets[:]))
-        turn_values(0, v_row0)
-
-        nc.vector.tensor_copy(k_bf[:, :, PACK - 1], k_win[PACK - 1][:].indirect(offsets[:]))
-        half = N // 2
-        for h in range(2):
-            cols = slice(h * half, (h + 1) * half)
-            nc.vector.quantize_mx(
-                k_codes[:, cols].bitcast(FP8X4), k_scales[:, cols], k_bf[:, cols, :].rearrange("p n j -> p (n j)")
-            )
+        q_bf = keep.tile([P, NQ, PACK], BF16, name="q_bf", align_bytes=64)
+        q_codes = keep.tile([P, NQ], U32, name="q_codes", align_bytes=64)
+        q_scales = keep.tile([P, NQ], U8, name="q_scales", align_bytes=64)
+        nc.scalar.copy(
+            q_bf[:].rearrange("p (c i) j -> p c j i", i=4), q_raw[:].rearrange("p j (c i) -> p c j i", i=4)
+        )
+        nc.vector.quantize_mx(q_codes[:].bitcast(FP8X4), q_scales[:], q_bf[:].rearrange("p q j -> p (q j)"))
 
         a_t = keep.tile([P, SB, NQ], F32, name="a_t")
         for c in range(SB):
             cols = slice(c * P, (c + 1) * P)
-            score = psum.tile([P, NQ], F32, name=f"score{c}", tag=f"sum{c}")
+            score = flat(s_bank[c], NQ)
             nc.tensor.matmul_mx(
-                score[:], k_codes[:, cols].bitcast(FP8X4), k_scales[:, cols], q_codes[:].bitcast(FP8X4), q_scales[:],
+                score, k_codes[:, cols].bitcast(FP8X4), k_scales[:, cols], q_codes[:].bitcast(FP8X4), q_scales[:],
                 start=True, stop=True,
             )
-            nc.scalar.activation(a_t[:, c, :], score[:], ACT.Copy, scale=nks_col[:, c : c + 1])
+            nc.scalar.activation(a_t[:, c, :], score, ACT.Copy, scale=nks_col[:, c : c + 1])
+
+        groups = ((0, 1), (2,), (3,))
+        v_bf = [keep.tile([P, len(gs) * P, PACK], BF16, name=f"v_bf{h}", align_bytes=64) for h, gs in enumerate(groups)]
+
+        def turn_values(h, i):
+            g = groups[h][i]
+            v_row = keep.tile([P, 2, 16, 16], BF16, name=f"v_row{g}")
+            nc.vector.tensor_copy(v_row[:].rearrange("e u b x -> e b u x"), v_win[g][:].indirect(offsets[:]))
+            words = v_row[:].rearrange("e u b x -> e (u b x)").bitcast(F32)
+            v_t = v_bank[g % 2]
+            for u in range(2):
+                nc.tensor.transpose(v_t[:, u, :], words[:, u * P : (u + 1) * P], ident[:])
+            dst = v_bf[h][:].rearrange("s e t -> s (e t)").bitcast(F32).rearrange("s (e u) -> s e u", u=2)
+            nc.scalar.copy(dst[:, i * P : (i + 1) * P, :], v_t[:, 0:2, :].rearrange("s u e -> s e u"))
+
+        turn_values(0, 0)
 
         neg_m = keep.tile([P, QB], F32, name="neg_m")
-        total = [keep.tile([P, 1], F32, name=f"total{b}") for b in range(QB)]
+        part = keep.tile([P, 2, QB], F32, name="part")
+        total = keep.tile([P, QB], F32, name="total")
         inv = keep.tile([P, QB], F32, name="inv")
         w_codes = keep.tile([P, NQ], U32, name="w_codes", align_bytes=64)
         w_scales = keep.tile([P, NQ], U8, name="w_scales", align_bytes=64)
-        a_q = []
         for b in range(QB):
-            a_b = banks[b]
             for c in range(SB):
-                nc.tensor.transpose(a_b[:, c, :], a_t[:, c, b * P : (b + 1) * P], ident[:])
-            a_q.append(a_b)
+                nc.tensor.transpose(a_bank[b][:, c, :], a_t[:, c, b * P : (b + 1) * P], ident[:])
         p_sb = []
         for b in range(QB):
-            nc.vector.tensor_reduce(neg_m[:, b : b + 1], a_q[b][:].rearrange("q c s -> q (c s)"), AXIS_X, MIN)
+            nc.vector.tensor_reduce(neg_m[:, b : b + 1], flat(a_bank[b], N), AXIS_X, MIN)
             p_b = keep.tile([P, PACK, P], F32, name=f"p_sb{b}")
-            nc.scalar.activation(
-                p_b[:], a_q[b][:].rearrange("q c s -> q (c s)").rearrange("q (s t) -> q t s", t=PACK), ACT.Exp,
-                bias=neg_m[:, b : b + 1], scale=-1.0, accum_out=total[b][:],
-            )
+            dealt = flat(a_bank[b], N).rearrange("q (b u r e) -> q u e b r", u=2, r=8, e=2)
+            for u in range(2):
+                nc.scalar.activation(
+                    p_b[:, 2 * u : 2 * u + 2, :].rearrange("q e (b r) -> q e b r", r=8), dealt[:, u], ACT.Exp,
+                    bias=neg_m[:, b : b + 1], scale=-1.0, accum_out=part[:, u, b : b + 1],
+                )
             p_sb.append(p_b)
+        turn_values(0, 1)
+        w_bf = [keep.tile([P, P, PACK], BF16, name=f"w_bf{b}", align_bytes=64) for b in range(QB)]
         for b in range(QB):
-            p_t = banks[b + 2]
+            p_t = s_bank[b]
             for t in range(PACK):
                 nc.tensor.transpose(p_t[:, t, :], p_sb[b][:, t, :], ident[:])
-            w_bf = keep.tile([P, P, PACK], BF16, name=f"w_bf{b}", align_bytes=64)
             nc.vector.tensor_tensor(
-                w_bf[:], p_t[:].rearrange("s t q -> s q t"),
+                w_bf[b][:], p_t[:].rearrange("s t q -> s q t"),
                 vs_col[:].unsqueeze(1).to_broadcast([P, P, PACK]), MULT,
             )
+        nc.vector.tensor_tensor(total[:], part[:, 0, :], part[:, 1, :], ADD)
+        for b in range(QB):
             cols = slice(b * P, (b + 1) * P)
             nc.vector.quantize_mx(
-                w_codes[:, cols].bitcast(FP8X4), w_scales[:, cols], w_bf[:].rearrange("s q t -> s (q t)")
+                w_codes[:, cols].bitcast(FP8X4), w_scales[:, cols], w_bf[b][:].rearrange("s q t -> s (q t)")
             )
-            nc.vector.reciprocal(inv[:, b : b + 1], total[b][:])
+        nc.vector.reciprocal(inv[:], total[:])
 
-        v_rows = [
-            v_row0[:],
-            a_t[:, 2:4, :].rearrange("s c q -> s (c q)"),
-            p_sb[1][:].rearrange("q t s -> q (t s)"),
-            p_sb[0][:].rearrange("q t s -> q (t s)"),
-        ]
-        for g in range(1, EB):
-            nc.vector.tensor_copy(v_rows[g], v_win[g][:].indirect(offsets[:]))
-        half_e = 2 * P
-        for h in range(2):
-            v_codes = keep.tile([P, half_e], U32, name=f"v_codes{h}", align_bytes=64)
-            v_scales = keep.tile([P, half_e], U8, name=f"v_scales{h}", align_bytes=64)
-            for g in (1,) if h == 0 else (2, 3):
-                turn_values(g, v_rows[g])
+        out_q = out[0].rearrange("(b q) e -> q b e", q=P)
+        y_banks = (s_bank[2:4], a_bank, s_bank[0:2])
+        for h, gs in enumerate(groups):
+            width = len(gs) * P
+            e_cols = slice(gs[0] * P, gs[0] * P + width)
+            last = h == len(groups) - 1
+            if h > 0:
+                turn_values(h, 0)
+            v_codes = keep.tile([P, width], U32, name=f"v_codes{h}", align_bytes=64)
+            v_scales = keep.tile([P, width], U8, name=f"v_scales{h}", align_bytes=64)
             nc.vector.quantize_mx(v_codes[:].bitcast(FP8X4), v_scales[:], v_bf[h][:].rearrange("s e t -> s (e t)"))
+            y_sb = keep.tile([P, QB, width], F32, name=f"y_sb{h}")
             for b in range(QB):
                 cols = slice(b * P, (b + 1) * P)
-                y = psum.tile([P, half_e], F32, name=f"y{h}_{b}", tag=f"sum{2 * h + b}")
+                y = flat(y_banks[h][b], width)
                 nc.tensor.matmul_mx(
-                    y[:], w_codes[:, cols].bitcast(FP8X4), w_scales[:, cols], v_codes[:].bitcast(FP8X4), v_scales[:],
+                    y, w_codes[:, cols].bitcast(FP8X4), w_scales[:, cols], v_codes[:].bitcast(FP8X4), v_scales[:],
                     start=True, stop=True,
                 )
-                y_sb = keep.tile([P, half_e], F32, name=f"y_sb{h}_{b}")
-                if h == 1 and b == 0:
-                    nc.vector.tensor_scalar(y_sb[:], y[:], inv[:, b : b + 1], None, MULT)
+                if last and b == 0:
+                    nc.vector.tensor_scalar(y_sb[:, b, :], y, inv[:, b : b + 1], None, MULT)
+                    nc.sync.dma_start(out_q[:, b, e_cols], y_sb[:, b, :])
                 else:
-                    nc.scalar.activation(y_sb[:], y[:], ACT.Copy, scale=inv[:, b : b + 1])
-                queue = nc.scalar if h == 1 and b == 1 else nc.sync
-                queue.dma_start(out[0, cols, h * half_e : (h + 1) * half_e], y_sb[:])
+                    nc.scalar.activation(y_sb[:, b, :], y, ACT.Copy, scale=inv[:, b : b + 1])
+            if last:
+                nc.scalar.dma_start(out_q[:, 1, e_cols], y_sb[:, 1, :])
+            else:
+                nc.sync.dma_start(out_q[:, :, e_cols], y_sb[:])

@@ -14,7 +14,6 @@ U8 = mybir.dt.uint8
 FP8X4 = mybir.dt.float8_e4m3fn_x4
 MULT = mybir.AluOpType.mult
 MIN = mybir.AluOpType.min
-ADD = mybir.AluOpType.add
 AXIS_X = mybir.AxisListType.X
 ACT = mybir.ActivationFunctionType
 
@@ -38,23 +37,24 @@ def tile_attend_mqa_topk_ks_kernel(tc, qT, kT, vT, ks, vs, offs, out):
         offsets = keep.tile([P, N // 16], U16, name="offsets")
         q_raw = keep.tile([P, PACK, NQ], F32, name="q_raw")
         k_win = [keep.tile([P, T], F32, name=f"k_win{t}") for t in range(PACK)]
-        v_win = [keep.tile([P, T], F32, name=f"v_win{g}") for g in range(EB)]
+        v_win = [keep.tile([P, T], F32, name=f"v_win{g}", tag=f"v_win{g}", align_bytes=64) for g in range(EB)]
         ks_win = keep.tile([P, T], F32, name="ks_win")
         vs_win = keep.tile([P, T], F32, name="vs_win")
 
         k_planes = kT.rearrange("(p j) n -> j p n", j=PACK)
         v_planes = vT.rearrange("(g e) n -> g e n", e=P)
         nc.sync.dma_start(offsets[:], offs)
-        for t in range(PACK):
+        split = 1280
+        for t, (win, row) in enumerate(((vs_win, vs), (ks_win, ks))):
+            nc.sync.dma_start(k_win[t][:], k_planes[t])
+            nc.vector.memset(win[:, 0:split], 0.0)
+            nc.gpsimd.memset(win[:, split:T], 0.0)
+            nc.sync.dma_start(win[0:1, :], row[0:1, :])
+        for t in (2, 3):
             nc.sync.dma_start(k_win[t][:], k_planes[t])
         nc.sync.dma_start(q_raw[:], qT[0].rearrange("(p j) q -> p j q", j=PACK))
         for g in range(EB):
             nc.sync.dma_start(v_win[g][:], v_planes[g])
-        split = 1280
-        for win, row in ((vs_win, vs), (ks_win, ks)):
-            nc.vector.memset(win[:, 0:split], 0.0)
-            nc.gpsimd.memset(win[:, split:T], 0.0)
-            nc.scalar.dma_start(win[0:1, :], row[0:1, :])
 
         warm = keep.tile([P, 1], F32, name="warm")
         nc.vector.memset(warm[:], 0.0)
@@ -75,7 +75,7 @@ def tile_attend_mqa_topk_ks_kernel(tc, qT, kT, vT, ks, vs, offs, out):
         k_scales = keep.tile([P, N], U8, name="k_scales", align_bytes=64)
         k_pair = keep.tile([P, 2, N], F32, name="k_pair")
         vs_row = keep.tile([P, N], F32, name="vs_row")
-        vs_dealt = keep.tile([P, PACK, P], F32, name="vs_dealt")
+        vs_all = keep.tile([P, N], F32, name="vs_all")
         ks_row = keep.tile([P, N], F32, name="ks_row")
         nks_col = keep.tile([P, SB], F32, name="nks_col")
         vs_col = keep.tile([P, PACK], F32, name="vs_col")
@@ -84,13 +84,12 @@ def tile_attend_mqa_topk_ks_kernel(tc, qT, kT, vT, ks, vs, offs, out):
         nc.vector.tensor_copy(vs_row[:], vs_win[:].indirect(offsets[:]))
         nc.vector.tensor_copy(k_pair[:, 1, :], k_win[1][:].indirect(offsets[:]))
         nc.vector.tensor_copy(ks_row[:], ks_win[:].indirect(offsets[:]))
-        nc.scalar.copy(
-            vs_dealt[:].rearrange("p (u e) (b r) -> p u e b r", u=2, r=8),
-            vs_row[:].rearrange("p (b u r e) -> p u e b r", u=2, r=8, e=2),
-        )
-        for t in range(PACK):
-            nc.tensor.transpose(a_bank[1][:, t, :], vs_dealt[:, t, :], ident[:])
+        for c in range(SB):
+            nc.tensor.transpose(a_bank[1][:, c, :], vs_row[:, c * P : (c + 1) * P], ident[:])
         nc.scalar.copy(vs_col[:], a_bank[1][:, :, 0])
+        for c in range(SB):
+            nc.tensor.transpose(v_bank[1][:, c, :], vs_col[:, c : c + 1].to_broadcast([P, P]), ident[:])
+        nc.scalar.copy(vs_all[:], flat(v_bank[1], N))
         nc.scalar.copy(k_bf[:, :, 0:2], k_pair[:].rearrange("p j n -> p n j"))
         for c in range(SB):
             nc.tensor.transpose(a_bank[0][:, c, :], ks_row[:, c * P : (c + 1) * P], ident[:])
@@ -117,85 +116,76 @@ def tile_attend_mqa_topk_ks_kernel(tc, qT, kT, vT, ks, vs, offs, out):
             )
             nc.scalar.activation(a_t[:, c, :], score, ACT.Copy, scale=nks_col[:, c : c + 1])
 
-        groups = ((0, 1), (2,), (3,))
-        v_bf = [keep.tile([P, len(gs) * P, PACK], BF16, name=f"v_bf{h}", align_bytes=64) for h, gs in enumerate(groups)]
+        first = keep.tile([P, NQ + 2 * P, PACK], BF16, name="first", align_bytes=64)
+        second = keep.tile([P, 2 * P, PACK], BF16, name="second", align_bytes=64)
 
-        def turn_values(h, i):
-            g = groups[h][i]
+        def turn(row, bank, dst, col):
+            words = row[:].rearrange("e u b x -> e (u b x)").bitcast(F32)
+            for u in range(2):
+                nc.tensor.transpose(bank[:, u, :], words[:, u * P : (u + 1) * P], ident[:])
+            pairs = dst[:].rearrange("s e t -> s (e t)").bitcast(F32).rearrange("s (e u) -> s e u", u=2)
+            nc.scalar.copy(pairs[:, col : col + P, :], bank[:, 0:2, :].rearrange("s u e -> s e u"))
+
+        def values(g):
             v_row = keep.tile([P, 2, 16, 16], BF16, name=f"v_row{g}")
             nc.vector.tensor_copy(v_row[:].rearrange("e u b x -> e b u x"), v_win[g][:].indirect(offsets[:]))
-            words = v_row[:].rearrange("e u b x -> e (u b x)").bitcast(F32)
-            v_t = v_bank[g % 2]
-            for u in range(2):
-                nc.tensor.transpose(v_t[:, u, :], words[:, u * P : (u + 1) * P], ident[:])
-            dst = v_bf[h][:].rearrange("s e t -> s (e t)").bitcast(F32).rearrange("s (e u) -> s e u", u=2)
-            nc.scalar.copy(dst[:, i * P : (i + 1) * P, :], v_t[:, 0:2, :].rearrange("s u e -> s e u"))
+            if g < 2:
+                turn(v_row, v_bank[g % 2], first, NQ + g * P)
+            else:
+                turn(v_row, v_bank[g % 2], second, (g - 2) * P)
 
-        turn_values(0, 0)
+        values(0)
 
         neg_m = keep.tile([P, QB], F32, name="neg_m")
-        part = keep.tile([P, 2, QB], F32, name="part")
         total = keep.tile([P, QB], F32, name="total")
         inv = keep.tile([P, QB], F32, name="inv")
-        w_codes = keep.tile([P, NQ], U32, name="w_codes", align_bytes=64)
-        w_scales = keep.tile([P, NQ], U8, name="w_scales", align_bytes=64)
         for b in range(QB):
             for c in range(SB):
                 nc.tensor.transpose(a_bank[b][:, c, :], a_t[:, c, b * P : (b + 1) * P], ident[:])
         p_sb = []
         for b in range(QB):
             nc.vector.tensor_reduce(neg_m[:, b : b + 1], flat(a_bank[b], N), AXIS_X, MIN)
-            p_b = keep.tile([P, PACK, P], F32, name=f"p_sb{b}")
-            dealt = flat(a_bank[b], N).rearrange("q (b u r e) -> q u e b r", u=2, r=8, e=2)
-            for u in range(2):
-                nc.scalar.activation(
-                    p_b[:, 2 * u : 2 * u + 2, :].rearrange("q e (b r) -> q e b r", r=8), dealt[:, u], ACT.Exp,
-                    bias=neg_m[:, b : b + 1], scale=-1.0, accum_out=part[:, u, b : b + 1],
-                )
+            p_b = keep.tile([P, N], F32, name=f"p_sb{b}")
+            nc.scalar.activation(
+                p_b[:], flat(a_bank[b], N), ACT.Exp,
+                bias=neg_m[:, b : b + 1], scale=-1.0, accum_out=total[:, b : b + 1],
+            )
             p_sb.append(p_b)
-        turn_values(0, 1)
-        w_bf = [keep.tile([P, P, PACK], BF16, name=f"w_bf{b}", align_bytes=64) for b in range(QB)]
+        values(1)
         for b in range(QB):
-            p_t = s_bank[b]
-            for t in range(PACK):
-                nc.tensor.transpose(p_t[:, t, :], p_sb[b][:, t, :], ident[:])
+            w_row = keep.tile([P, 2, 16, 16], BF16, name=f"w_row{b}")
             nc.vector.tensor_tensor(
-                w_bf[b][:], p_t[:].rearrange("s t q -> s q t"),
-                vs_col[:].unsqueeze(1).to_broadcast([P, P, PACK]), MULT,
+                w_row[:].rearrange("q u b x -> q b u x"),
+                p_sb[b][:].rearrange("q (b u x) -> q b u x", u=2, x=16),
+                vs_all[:].rearrange("q (b u x) -> q b u x", u=2, x=16), MULT,
             )
-        nc.vector.tensor_tensor(total[:], part[:, 0, :], part[:, 1, :], ADD)
-        for b in range(QB):
-            cols = slice(b * P, (b + 1) * P)
-            nc.vector.quantize_mx(
-                w_codes[:, cols].bitcast(FP8X4), w_scales[:, cols], w_bf[b][:].rearrange("s q t -> s (q t)")
-            )
+            turn(w_row, s_bank[b], first, b * P)
         nc.vector.reciprocal(inv[:], total[:])
+        values(2)
+        values(3)
 
-        out_q = out[0].rearrange("(b q) e -> q b e", q=P)
-        y_banks = (s_bank[2:4], a_bank, s_bank[0:2])
-        for h, gs in enumerate(groups):
-            width = len(gs) * P
-            e_cols = slice(gs[0] * P, gs[0] * P + width)
-            last = h == len(groups) - 1
-            if h > 0:
-                turn_values(h, 0)
-            v_codes = keep.tile([P, width], U32, name=f"v_codes{h}", align_bytes=64)
-            v_scales = keep.tile([P, width], U8, name=f"v_scales{h}", align_bytes=64)
-            nc.vector.quantize_mx(v_codes[:].bitcast(FP8X4), v_scales[:], v_bf[h][:].rearrange("s e t -> s (e t)"))
-            y_sb = keep.tile([P, QB, width], F32, name=f"y_sb{h}")
+        codes1 = keep.tile([P, NQ + 2 * P], U32, name="codes1", tag="v_win3", align_bytes=64)
+        scales1 = keep.tile([P, NQ + 2 * P], U8, name="scales1", align_bytes=64)
+        codes2 = keep.tile([P, 2 * P], U32, name="codes2", align_bytes=64)
+        scales2 = keep.tile([P, 2 * P], U8, name="scales2", align_bytes=64)
+        nc.vector.quantize_mx(codes1[:].bitcast(FP8X4), scales1[:], first[:].rearrange("s e t -> s (e t)"))
+        nc.vector.quantize_mx(codes2[:].bitcast(FP8X4), scales2[:], second[:].rearrange("s e t -> s (e t)"))
+
+        y_banks = (s_bank[2:4], a_bank)
+        halves = ((codes1[:, NQ:], scales1[:, NQ:]), (codes2[:], scales2[:]))
+        for h, (v_codes, v_scales) in enumerate(halves):
+            e_cols = slice(h * 2 * P, (h + 1) * 2 * P)
             for b in range(QB):
                 cols = slice(b * P, (b + 1) * P)
-                y = flat(y_banks[h][b], width)
+                y = flat(y_banks[h][b], 2 * P)
                 nc.tensor.matmul_mx(
-                    y, w_codes[:, cols].bitcast(FP8X4), w_scales[:, cols], v_codes[:].bitcast(FP8X4), v_scales[:],
+                    y, codes1[:, cols].bitcast(FP8X4), scales1[:, cols], v_codes.bitcast(FP8X4), v_scales,
                     start=True, stop=True,
                 )
-                if last and b == 0:
-                    nc.vector.tensor_scalar(y_sb[:, b, :], y, inv[:, b : b + 1], None, MULT)
-                    nc.sync.dma_start(out_q[:, b, e_cols], y_sb[:, b, :])
+                y_sb = keep.tile([P, 2 * P], F32, name=f"y_sb{h}_{b}")
+                if b == 1:
+                    nc.vector.tensor_scalar(y_sb[:], y, inv[:, b : b + 1], None, MULT)
                 else:
-                    nc.scalar.activation(y_sb[:, b, :], y, ACT.Copy, scale=inv[:, b : b + 1])
-            if last:
-                nc.scalar.dma_start(out_q[:, 1, e_cols], y_sb[:, 1, :])
-            else:
-                nc.sync.dma_start(out_q[:, :, e_cols], y_sb[:])
+                    nc.scalar.activation(y_sb[:], y, ACT.Copy, scale=inv[:, b : b + 1])
+                queue = nc.scalar if h == 1 and b == 0 else nc.sync
+                queue.dma_start(out[0, cols, e_cols], y_sb[:])

@@ -101,26 +101,36 @@ def tile_attend_mqa_topk_ks_kernel(tc, qT, kT, vT, ks, vs, offs, out):
         q_bf = keep.tile([P, NQ, PACK], BF16, name="q_bf", align_bytes=64)
         q_codes = keep.tile([P, NQ], U32, name="q_codes", align_bytes=64)
         q_scales = keep.tile([P, NQ], U8, name="q_scales", align_bytes=64)
-        nc.scalar.copy(
-            q_bf[:].rearrange("p (c i) j -> p c j i", i=4), q_raw[:].rearrange("p j (c i) -> p c j i", i=4)
-        )
-        nc.vector.quantize_mx(q_codes[:].bitcast(FP8X4), q_scales[:], q_bf[:].rearrange("p q j -> p (q j)"))
-
-        a_t = keep.tile([P, SB, NQ], F32, name="a_t")
-        for c in range(SB):
-            cols = slice(c * P, (c + 1) * P)
-            score = flat(s_bank[c], NQ)
-            nc.tensor.matmul_mx(
-                score, k_codes[:, cols].bitcast(FP8X4), k_scales[:, cols], q_codes[:].bitcast(FP8X4), q_scales[:],
-                start=True, stop=True,
+        for b in range(QB):
+            rows = slice(b * P, (b + 1) * P)
+            nc.scalar.copy(
+                q_bf[:, rows, :].rearrange("p (c i) j -> p c j i", i=4),
+                q_raw[:, :, rows].rearrange("p j (c i) -> p c j i", i=4),
             )
-            nc.scalar.activation(a_t[:, c, :], score, ACT.Copy, scale=nks_col[:, c : c + 1])
+            nc.vector.quantize_mx(
+                q_codes[:, rows].bitcast(FP8X4), q_scales[:, rows], q_bf[:, rows, :].rearrange("p q j -> p (q j)")
+            )
+
+        a_t = [keep.tile([P, SB, P], F32, name=f"a_t{b}") for b in range(QB)]
+        for b in range(QB):
+            rows = slice(b * P, (b + 1) * P)
+            for c in range(SB):
+                cols = slice(c * P, (c + 1) * P)
+                nc.tensor.matmul_mx(
+                    s_bank[2 * b + c // 2][:, c % 2, :], k_codes[:, cols].bitcast(FP8X4), k_scales[:, cols],
+                    q_codes[:, rows].bitcast(FP8X4), q_scales[:, rows], start=True, stop=True,
+                )
+        for b in range(QB):
+            for c in range(SB):
+                nc.scalar.activation(
+                    a_t[b][:, c, :], s_bank[2 * b + c // 2][:, c % 2, :], ACT.Copy, scale=nks_col[:, c : c + 1]
+                )
 
         first = keep.tile([P, NQ + 2 * P, PACK], BF16, name="first", align_bytes=64)
-        second = keep.tile([P, 2 * P, PACK], BF16, name="second", align_bytes=64)
+        late = [keep.tile([P, P, PACK], BF16, name=f"late{g}", align_bytes=64) for g in range(2)]
 
         def turn(row, bank, dst, col):
-            words = row[:].rearrange("e u b x -> e (u b x)").bitcast(F32)
+            words = row.rearrange("e u b x -> e (u b x)").bitcast(F32)
             for u in range(2):
                 nc.tensor.transpose(bank[:, u, :], words[:, u * P : (u + 1) * P], ident[:])
             pairs = dst[:].rearrange("s e t -> s (e t)").bitcast(F32).rearrange("s (e u) -> s e u", u=2)
@@ -130,9 +140,9 @@ def tile_attend_mqa_topk_ks_kernel(tc, qT, kT, vT, ks, vs, offs, out):
             v_row = keep.tile([P, 2, 16, 16], BF16, name=f"v_row{g}")
             nc.vector.tensor_copy(v_row[:].rearrange("e u b x -> e b u x"), v_win[g][:].indirect(offsets[:]))
             if g < 2:
-                turn(v_row, v_bank[g % 2], first, NQ + g * P)
+                turn(v_row[:], v_bank[g % 2], first, NQ + g * P)
             else:
-                turn(v_row, v_bank[g % 2], second, (g - 2) * P)
+                turn(v_row[:], v_bank[g % 2], late[g - 2], 0)
 
         values(0)
 
@@ -141,7 +151,7 @@ def tile_attend_mqa_topk_ks_kernel(tc, qT, kT, vT, ks, vs, offs, out):
         inv = keep.tile([P, QB], F32, name="inv")
         for b in range(QB):
             for c in range(SB):
-                nc.tensor.transpose(a_bank[b][:, c, :], a_t[:, c, b * P : (b + 1) * P], ident[:])
+                nc.tensor.transpose(a_bank[b][:, c, :], a_t[b][:, c, :], ident[:])
         p_sb = []
         for b in range(QB):
             nc.vector.tensor_reduce(neg_m[:, b : b + 1], flat(a_bank[b], N), AXIS_X, MIN)
@@ -152,10 +162,11 @@ def tile_attend_mqa_topk_ks_kernel(tc, qT, kT, vT, ks, vs, offs, out):
             )
             p_sb.append(p_b)
         values(1)
+        w_rows = keep.tile([P, QB, 2, 16, 16], BF16, name="w_rows", tag="v_win1", align_bytes=64)
         for b in range(QB):
-            w_row = keep.tile([P, 2, 16, 16], BF16, name=f"w_row{b}")
+            w_row = w_rows[:, b]
             nc.vector.tensor_tensor(
-                w_row[:].rearrange("q u b x -> q b u x"),
+                w_row.rearrange("q u b x -> q b u x"),
                 p_sb[b][:].rearrange("q (b u x) -> q b u x", u=2, x=16),
                 vs_all[:].rearrange("q (b u x) -> q b u x", u=2, x=16), MULT,
             )
@@ -163,29 +174,41 @@ def tile_attend_mqa_topk_ks_kernel(tc, qT, kT, vT, ks, vs, offs, out):
         nc.vector.reciprocal(inv[:], total[:])
         values(2)
         values(3)
-
-        codes1 = keep.tile([P, NQ + 2 * P], U32, name="codes1", tag="v_win3", align_bytes=64)
+        codes12 = keep.tile([P, NQ + 3 * P], U32, name="codes12", tag="v_win3", align_bytes=64)
+        codes1 = codes12[:, 0 : NQ + 2 * P]
         scales1 = keep.tile([P, NQ + 2 * P], U8, name="scales1", align_bytes=64)
-        codes2 = keep.tile([P, 2 * P], U32, name="codes2", align_bytes=64)
-        scales2 = keep.tile([P, 2 * P], U8, name="scales2", align_bytes=64)
-        nc.vector.quantize_mx(codes1[:].bitcast(FP8X4), scales1[:], first[:].rearrange("s e t -> s (e t)"))
-        nc.vector.quantize_mx(codes2[:].bitcast(FP8X4), scales2[:], second[:].rearrange("s e t -> s (e t)"))
+        nc.vector.quantize_mx(codes1.bitcast(FP8X4), scales1[:], first[:].rearrange("s e t -> s (e t)"))
 
-        y_banks = (s_bank[2:4], a_bank)
-        halves = ((codes1[:, NQ:], scales1[:, NQ:]), (codes2[:], scales2[:]))
-        for h, (v_codes, v_scales) in enumerate(halves):
-            e_cols = slice(h * 2 * P, (h + 1) * 2 * P)
+        def product(bank, b, v_codes, v_scales, width):
+            cols = slice(b * P, (b + 1) * P)
+            y = flat(bank, width)
+            nc.tensor.matmul_mx(
+                y, codes1[:, cols].bitcast(FP8X4), scales1[:, cols], v_codes.bitcast(FP8X4), v_scales,
+                start=True, stop=True,
+            )
+            return y
+
+        out_q = out[0].rearrange("(b q) e -> q b e", q=P)
+        for b in range(QB):
+            y = product(s_bank[2 + b], b, codes1[:, NQ:], scales1[:, NQ:], 2 * P)
+            y_sb = keep.tile([P, 2 * P], F32, name=f"y_first{b}")
+            nc.scalar.activation(y_sb[:], y, ACT.Copy, scale=inv[:, b : b + 1])
+            nc.sync.dma_start(out_q[:, b, 0 : 2 * P], y_sb[:])
+
+        codes3 = keep.tile([P, P], U32, name="codes3", align_bytes=64)
+        for g, codes, banks in ((2, codes12[:, NQ + 2 * P :], a_bank), (3, codes3[:], s_bank)):
+            scales = keep.tile([P, P], U8, name=f"scales{g}", align_bytes=64)
+            nc.vector.quantize_mx(codes.bitcast(FP8X4), scales[:], late[g - 2][:].rearrange("s e t -> s (e t)"))
+            y_sb = keep.tile([P, QB, P], F32, name=f"y_late{g}")
+            e_cols = slice(g * P, (g + 1) * P)
             for b in range(QB):
-                cols = slice(b * P, (b + 1) * P)
-                y = flat(y_banks[h][b], 2 * P)
-                nc.tensor.matmul_mx(
-                    y, codes1[:, cols].bitcast(FP8X4), scales1[:, cols], v_codes.bitcast(FP8X4), v_scales,
-                    start=True, stop=True,
-                )
-                y_sb = keep.tile([P, 2 * P], F32, name=f"y_sb{h}_{b}")
-                if b == 1:
-                    nc.vector.tensor_scalar(y_sb[:], y, inv[:, b : b + 1], None, MULT)
+                y = product(banks[b], b, codes, scales[:], P)
+                if g == 2 or b == 1:
+                    nc.vector.tensor_scalar(y_sb[:, b, :], y, inv[:, b : b + 1], None, MULT)
                 else:
-                    nc.scalar.activation(y_sb[:], y, ACT.Copy, scale=inv[:, b : b + 1])
-                queue = nc.scalar if h == 1 and b == 0 else nc.sync
-                queue.dma_start(out[0, cols, e_cols], y_sb[:])
+                    nc.scalar.activation(y_sb[:, b, :], y, ACT.Copy, scale=inv[:, b : b + 1])
+            if g == 2:
+                nc.sync.dma_start(out_q[:, :, e_cols], y_sb[:])
+            else:
+                nc.scalar.dma_start(out_q[:, 0, e_cols], y_sb[:, 0, :])
+                nc.sync.dma_start(out_q[:, 1, e_cols], y_sb[:, 1, :])

@@ -43,10 +43,11 @@ def tile_attend_mqa_topk_ks_kernel(tc, qT, kT, vT, ks, vs, offs, out):
 
         k_planes = kT.rearrange("(p j) n -> j p n", j=PACK)
         v_planes = vT.rearrange("(g e) n -> g e n", e=P)
-        nc.sync.dma_start(offsets[:], offs)
         split = 1280
         for t, (win, row) in enumerate(((vs_win, vs), (ks_win, ks))):
             nc.sync.dma_start(k_win[t][:], k_planes[t])
+            if t == 0:
+                nc.sync.dma_start(offsets[:], offs)
             nc.vector.memset(win[:, 0:split], 0.0)
             nc.gpsimd.memset(win[:, split:T], 0.0)
             nc.sync.dma_start(win[0:1, :], row[0:1, :])
@@ -130,15 +131,15 @@ def tile_attend_mqa_topk_ks_kernel(tc, qT, kT, vT, ks, vs, offs, out):
         late = [keep.tile([P, P, PACK], BF16, name=f"late{g}", align_bytes=64) for g in range(2)]
 
         def turn(row, bank, dst, col):
-            words = row.rearrange("e u b x -> e (u b x)").bitcast(F32)
+            words = row.bitcast(F32)
             for u in range(2):
-                nc.tensor.transpose(bank[:, u, :], words[:, u * P : (u + 1) * P], ident[:])
+                nc.tensor.transpose(bank[:, u, :], words[:, u::2], ident[:])
             pairs = dst[:].rearrange("s e t -> s (e t)").bitcast(F32).rearrange("s (e u) -> s e u", u=2)
             nc.scalar.copy(pairs[:, col : col + P, :], bank[:, 0:2, :].rearrange("s u e -> s e u"))
 
         def values(g):
-            v_row = keep.tile([P, 2, 16, 16], BF16, name=f"v_row{g}")
-            nc.vector.tensor_copy(v_row[:].rearrange("e u b x -> e b u x"), v_win[g][:].indirect(offsets[:]))
+            v_row = keep.tile([P, N], BF16, name=f"v_row{g}")
+            nc.vector.tensor_copy(v_row[:], v_win[g][:].indirect(offsets[:]))
             if g < 2:
                 turn(v_row[:], v_bank[g % 2], first, NQ + g * P)
             else:
@@ -162,15 +163,10 @@ def tile_attend_mqa_topk_ks_kernel(tc, qT, kT, vT, ks, vs, offs, out):
             )
             p_sb.append(p_b)
         values(1)
-        w_rows = keep.tile([P, QB, 2, 16, 16], BF16, name="w_rows", tag="v_win1", align_bytes=64)
         for b in range(QB):
-            w_row = w_rows[:, b]
-            nc.vector.tensor_tensor(
-                w_row.rearrange("q u b x -> q b u x"),
-                p_sb[b][:].rearrange("q (b u x) -> q b u x", u=2, x=16),
-                vs_all[:].rearrange("q (b u x) -> q b u x", u=2, x=16), MULT,
-            )
-            turn(w_row, s_bank[b], first, b * P)
+            w_row = keep.tile([P, N], BF16, name=f"w_row{b}")
+            nc.gpsimd.tensor_tensor(w_row[:], p_sb[b][:], vs_all[:], MULT)
+            turn(w_row[:], s_bank[b], first, b * P)
         nc.vector.reciprocal(inv[:], total[:])
         values(2)
         values(3)

@@ -43,13 +43,11 @@ def tile_attend_mqa_topk_ks_kernel(tc, qT, kT, vT, ks, vs, offs, out):
 
         k_planes = kT.rearrange("(p j) n -> j p n", j=PACK)
         v_planes = vT.rearrange("(g e) n -> g e n", e=P)
-        split = 1280
         for t, (win, row) in enumerate(((vs_win, vs), (ks_win, ks))):
             nc.sync.dma_start(k_win[t][:], k_planes[t])
             if t == 0:
                 nc.sync.dma_start(offsets[:], offs)
-            nc.vector.memset(win[:, 0:split], 0.0)
-            nc.gpsimd.memset(win[:, split:T], 0.0)
+            nc.vector.memset(win[:], 0.0)
             nc.sync.dma_start(win[0:1, :], row[0:1, :])
         for t in (2, 3):
             nc.sync.dma_start(k_win[t][:], k_planes[t])
@@ -127,23 +125,24 @@ def tile_attend_mqa_topk_ks_kernel(tc, qT, kT, vT, ks, vs, offs, out):
                     a_t[b][:, c, :], s_bank[2 * b + c // 2][:, c % 2, :], ACT.Copy, scale=nks_col[:, c : c + 1]
                 )
 
-        first = keep.tile([P, NQ + 2 * P, PACK], BF16, name="first", align_bytes=64)
+        w_bf = keep.tile([P, NQ, PACK], BF16, name="w_bf", align_bytes=64)
+        early = keep.tile([P, 2 * P, PACK], BF16, name="early", align_bytes=64)
         late = [keep.tile([P, P, PACK], BF16, name=f"late{g}", align_bytes=64) for g in range(2)]
 
-        def turn(row, bank, dst, col):
+        def turn(row, bank, dst, col, copy):
             words = row.bitcast(F32)
             for u in range(2):
                 nc.tensor.transpose(bank[:, u, :], words[:, u::2], ident[:])
             pairs = dst[:].rearrange("s e t -> s (e t)").bitcast(F32).rearrange("s (e u) -> s e u", u=2)
-            nc.scalar.copy(pairs[:, col : col + P, :], bank[:, 0:2, :].rearrange("s u e -> s e u"))
+            copy(pairs[:, col : col + P, :], bank[:, 0:2, :].rearrange("s u e -> s e u"))
 
         def values(g):
             v_row = keep.tile([P, N], BF16, name=f"v_row{g}")
             nc.vector.tensor_copy(v_row[:], v_win[g][:].indirect(offsets[:]))
             if g < 2:
-                turn(v_row[:], v_bank[g % 2], first, NQ + g * P)
+                turn(v_row[:], v_bank[g % 2], early, g * P, nc.scalar.copy)
             else:
-                turn(v_row[:], v_bank[g % 2], late[g - 2], 0)
+                turn(v_row[:], s_bank[g - 2], late[g - 2], 0, nc.scalar.copy if g == 2 else nc.vector.tensor_copy)
 
         values(0)
 
@@ -166,45 +165,43 @@ def tile_attend_mqa_topk_ks_kernel(tc, qT, kT, vT, ks, vs, offs, out):
         for b in range(QB):
             w_row = keep.tile([P, N], BF16, name=f"w_row{b}")
             nc.gpsimd.tensor_tensor(w_row[:], p_sb[b][:], vs_all[:], MULT)
-            turn(w_row[:], s_bank[b], first, b * P)
+            turn(w_row[:], v_bank[1], w_bf, b * P, nc.scalar.copy)
         nc.vector.reciprocal(inv[:], total[:])
         values(2)
+        early_codes = keep.tile([P, 2 * P], U32, name="early_codes", tag="v_win2", align_bytes=64)
+        early_scales = keep.tile([P, 2 * P], U8, name="early_scales", align_bytes=64)
+        nc.vector.quantize_mx(early_codes[:].bitcast(FP8X4), early_scales[:], early[:].rearrange("s e t -> s (e t)"))
         values(3)
-        codes12 = keep.tile([P, NQ + 3 * P], U32, name="codes12", tag="v_win3", align_bytes=64)
-        codes1 = codes12[:, 0 : NQ + 2 * P]
-        scales1 = keep.tile([P, NQ + 2 * P], U8, name="scales1", align_bytes=64)
-        nc.vector.quantize_mx(codes1.bitcast(FP8X4), scales1[:], first[:].rearrange("s e t -> s (e t)"))
+        held = keep.tile([P, NQ + P], U32, name="held", tag="v_win3", align_bytes=64)
+        w_codes = held[:, 0:NQ]
+        w_scales = keep.tile([P, NQ], U8, name="w_scales", align_bytes=64)
+        nc.vector.quantize_mx(w_codes.bitcast(FP8X4), w_scales[:], w_bf[:].rearrange("s e t -> s (e t)"))
 
-        def product(bank, b, v_codes, v_scales, width):
+        def product(bank, b, v_codes, v_scales, width, y_sb, on_vector):
             cols = slice(b * P, (b + 1) * P)
             y = flat(bank, width)
             nc.tensor.matmul_mx(
-                y, codes1[:, cols].bitcast(FP8X4), scales1[:, cols], v_codes.bitcast(FP8X4), v_scales,
+                y, w_codes[:, cols].bitcast(FP8X4), w_scales[:, cols], v_codes.bitcast(FP8X4), v_scales,
                 start=True, stop=True,
             )
-            return y
+            if on_vector:
+                nc.vector.tensor_scalar(y_sb, y, inv[:, b : b + 1], None, MULT)
+            else:
+                nc.scalar.activation(y_sb, y, ACT.Copy, scale=inv[:, b : b + 1])
 
         out_q = out[0].rearrange("(b q) e -> q b e", q=P)
         for b in range(QB):
-            y = product(s_bank[2 + b], b, codes1[:, NQ:], scales1[:, NQ:], 2 * P)
-            y_sb = keep.tile([P, 2 * P], F32, name=f"y_first{b}")
-            nc.scalar.activation(y_sb[:], y, ACT.Copy, scale=inv[:, b : b + 1])
+            y_sb = keep.tile([P, 2 * P], F32, name=f"y_early{b}")
+            product(s_bank[2 + b], b, early_codes[:], early_scales[:], 2 * P, y_sb[:], False)
             nc.sync.dma_start(out_q[:, b, 0 : 2 * P], y_sb[:])
 
         codes3 = keep.tile([P, P], U32, name="codes3", align_bytes=64)
-        for g, codes, banks in ((2, codes12[:, NQ + 2 * P :], a_bank), (3, codes3[:], s_bank)):
+        for g, codes, banks in ((2, held[:, NQ:], a_bank), (3, codes3[:], s_bank)):
             scales = keep.tile([P, P], U8, name=f"scales{g}", align_bytes=64)
             nc.vector.quantize_mx(codes.bitcast(FP8X4), scales[:], late[g - 2][:].rearrange("s e t -> s (e t)"))
             y_sb = keep.tile([P, QB, P], F32, name=f"y_late{g}")
             e_cols = slice(g * P, (g + 1) * P)
             for b in range(QB):
-                y = product(banks[b], b, codes, scales[:], P)
-                if g == 2 or b == 1:
-                    nc.vector.tensor_scalar(y_sb[:, b, :], y, inv[:, b : b + 1], None, MULT)
-                else:
-                    nc.scalar.activation(y_sb[:, b, :], y, ACT.Copy, scale=inv[:, b : b + 1])
-            if g == 2:
-                nc.sync.dma_start(out_q[:, :, e_cols], y_sb[:])
-            else:
-                nc.scalar.dma_start(out_q[:, 0, e_cols], y_sb[:, 0, :])
-                nc.sync.dma_start(out_q[:, 1, e_cols], y_sb[:, 1, :])
+                product(banks[b], b, codes, scales[:], P, y_sb[:, b, :], g == 3)
+            queue = nc.scalar if g == 2 else nc.sync
+            queue.dma_start(out_q[:, :, e_cols], y_sb[:])

@@ -14,6 +14,7 @@ U8 = mybir.dt.uint8
 FP8X4 = mybir.dt.float8_e4m3fn_x4
 MULT = mybir.AluOpType.mult
 MIN = mybir.AluOpType.min
+ADD = mybir.AluOpType.add
 AXIS_X = mybir.AxisListType.X
 ACT = mybir.ActivationFunctionType
 
@@ -48,7 +49,10 @@ def tile_attend_mqa_topk_ks_kernel(tc, qT, kT, vT, ks, vs, offs, out):
             if t == 0:
                 nc.sync.dma_start(offsets[:], offs)
             nc.vector.memset(win[:], 0.0)
-            nc.sync.dma_start(win[0:1, :], row[0:1, :])
+            for h in range(2):
+                part = slice(64 * t + 4 * h, 64 * t + 4 * h + 1)
+                cols = slice(h * T // 2, (h + 1) * T // 2)
+                nc.sync.dma_start(win[part, cols], row[part, cols])
         for t in (2, 3):
             nc.sync.dma_start(k_win[t][:], k_planes[t])
         nc.sync.dma_start(q_raw[:], qT[0].rearrange("(p j) q -> p j q", j=PACK))
@@ -69,6 +73,12 @@ def tile_attend_mqa_topk_ks_kernel(tc, qT, kT, vT, ks, vs, offs, out):
         def flat(bank, width):
             return bank[:].rearrange("p c s -> p (c s)")[:, 0:width]
 
+        def dealt(row):
+            return row.rearrange("p (u b x) -> p b u x", u=2, x=16)
+
+        def in_order(row):
+            return row.rearrange("p (b u x) -> p b u x", u=2, x=16)
+
         k_bf = keep.tile([P, N, PACK], BF16, name="k_bf", align_bytes=64)
         k_codes = keep.tile([P, N], U32, name="k_codes", align_bytes=64)
         k_scales = keep.tile([P, N], U8, name="k_scales", align_bytes=64)
@@ -85,14 +95,14 @@ def tile_attend_mqa_topk_ks_kernel(tc, qT, kT, vT, ks, vs, offs, out):
         nc.vector.tensor_copy(ks_row[:], ks_win[:].indirect(offsets[:]))
         for c in range(SB):
             nc.tensor.transpose(a_bank[1][:, c, :], vs_row[:, c * P : (c + 1) * P], ident[:])
-        nc.scalar.copy(vs_col[:], a_bank[1][:, :, 0])
+        nc.vector.tensor_reduce(vs_col[:], a_bank[1][:, :, 0:8:4], AXIS_X, ADD)
         for c in range(SB):
             nc.tensor.transpose(v_bank[1][:, c, :], vs_col[:, c : c + 1].to_broadcast([P, P]), ident[:])
-        nc.scalar.copy(vs_all[:], flat(v_bank[1], N))
+        nc.scalar.copy(dealt(vs_all[:]), in_order(flat(v_bank[1], N)))
         nc.scalar.copy(k_bf[:, :, 0:2], k_pair[:].rearrange("p j n -> p n j"))
         for c in range(SB):
             nc.tensor.transpose(a_bank[0][:, c, :], ks_row[:, c * P : (c + 1) * P], ident[:])
-        nc.scalar.activation(nks_col[:], a_bank[0][:, :, 0], ACT.Copy, scale=-1.0)
+        nc.vector.tensor_reduce(nks_col[:], a_bank[0][:, :, 64:72:4], AXIS_X, ADD, negate=True)
         for t in (2, 3):
             nc.vector.tensor_copy(k_bf[:, :, t], k_win[t][:].indirect(offsets[:]))
         nc.vector.quantize_mx(k_codes[:].bitcast(FP8X4), k_scales[:], k_bf[:].rearrange("p n j -> p (n j)"))
@@ -132,13 +142,13 @@ def tile_attend_mqa_topk_ks_kernel(tc, qT, kT, vT, ks, vs, offs, out):
         def turn(row, bank, dst, col, copy):
             words = row.bitcast(F32)
             for u in range(2):
-                nc.tensor.transpose(bank[:, u, :], words[:, u::2], ident[:])
+                nc.tensor.transpose(bank[:, u, :], words[:, u * P : (u + 1) * P], ident[:])
             pairs = dst[:].rearrange("s e t -> s (e t)").bitcast(F32).rearrange("s (e u) -> s e u", u=2)
             copy(pairs[:, col : col + P, :], bank[:, 0:2, :].rearrange("s u e -> s e u"))
 
         def values(g):
             v_row = keep.tile([P, N], BF16, name=f"v_row{g}")
-            nc.vector.tensor_copy(v_row[:], v_win[g][:].indirect(offsets[:]))
+            nc.vector.tensor_copy(dealt(v_row[:]), v_win[g][:].indirect(offsets[:]))
             if g < 2:
                 turn(v_row[:], v_bank[g % 2], early, g * P, nc.scalar.copy)
             else:
@@ -157,7 +167,7 @@ def tile_attend_mqa_topk_ks_kernel(tc, qT, kT, vT, ks, vs, offs, out):
             nc.vector.tensor_reduce(neg_m[:, b : b + 1], flat(a_bank[b], N), AXIS_X, MIN)
             p_b = keep.tile([P, N], F32, name=f"p_sb{b}")
             nc.scalar.activation(
-                p_b[:], flat(a_bank[b], N), ACT.Exp,
+                dealt(p_b[:]), in_order(flat(a_bank[b], N)), ACT.Exp,
                 bias=neg_m[:, b : b + 1], scale=-1.0, accum_out=total[:, b : b + 1],
             )
             p_sb.append(p_b)

@@ -14,7 +14,6 @@ U8 = mybir.dt.uint8
 FP8X4 = mybir.dt.float8_e4m3fn_x4
 MULT = mybir.AluOpType.mult
 MIN = mybir.AluOpType.min
-ADD = mybir.AluOpType.add
 AXIS_X = mybir.AxisListType.X
 ACT = mybir.ActivationFunctionType
 
@@ -49,10 +48,7 @@ def tile_attend_mqa_topk_ks_kernel(tc, qT, kT, vT, ks, vs, offs, out):
             if t == 0:
                 nc.sync.dma_start(offsets[:], offs)
             nc.vector.memset(win[:], 0.0)
-            for h in range(2):
-                part = slice(64 * t + 4 * h, 64 * t + 4 * h + 1)
-                cols = slice(h * T // 2, (h + 1) * T // 2)
-                nc.sync.dma_start(win[part, cols], row[part, cols])
+            nc.sync.dma_start(win[64 * t : 64 * t + 1, :], row[0:1, :])
         for t in (2, 3):
             nc.sync.dma_start(k_win[t][:], k_planes[t])
         nc.sync.dma_start(q_raw[:], qT[0].rearrange("(p j) q -> p j q", j=PACK))
@@ -95,14 +91,14 @@ def tile_attend_mqa_topk_ks_kernel(tc, qT, kT, vT, ks, vs, offs, out):
         nc.vector.tensor_copy(ks_row[:], ks_win[:].indirect(offsets[:]))
         for c in range(SB):
             nc.tensor.transpose(a_bank[1][:, c, :], vs_row[:, c * P : (c + 1) * P], ident[:])
-        nc.vector.tensor_reduce(vs_col[:], a_bank[1][:, :, 0:8:4], AXIS_X, ADD)
+        nc.scalar.copy(vs_col[:], a_bank[1][:, :, 0])
         for c in range(SB):
             nc.tensor.transpose(v_bank[1][:, c, :], vs_col[:, c : c + 1].to_broadcast([P, P]), ident[:])
         nc.scalar.copy(dealt(vs_all[:]), in_order(flat(v_bank[1], N)))
         nc.scalar.copy(k_bf[:, :, 0:2], k_pair[:].rearrange("p j n -> p n j"))
         for c in range(SB):
             nc.tensor.transpose(a_bank[0][:, c, :], ks_row[:, c * P : (c + 1) * P], ident[:])
-        nc.vector.tensor_reduce(nks_col[:], a_bank[0][:, :, 64:72:4], AXIS_X, ADD, negate=True)
+        nc.scalar.activation(nks_col[:], a_bank[0][:, :, 64], ACT.Copy, scale=-1.0)
         for t in (2, 3):
             nc.vector.tensor_copy(k_bf[:, :, t], k_win[t][:].indirect(offsets[:]))
         nc.vector.quantize_mx(k_codes[:].bitcast(FP8X4), k_scales[:], k_bf[:].rearrange("p n j -> p (n j)"))

@@ -99,9 +99,14 @@ def tile_attend_mqa_topk_ks_kernel(tc, qT, kT, vT, ks, vs, offs, out):
         for c in range(SB):
             nc.tensor.transpose(a_bank[0][:, c, :], ks_row[:, c * P : (c + 1) * P], ident[:])
         nc.scalar.activation(nks_col[:], a_bank[0][:, :, 64], ACT.Copy, scale=-1.0)
-        for t in (2, 3):
-            nc.vector.tensor_copy(k_bf[:, :, t], k_win[t][:].indirect(offsets[:]))
-        nc.vector.quantize_mx(k_codes[:].bitcast(FP8X4), k_scales[:], k_bf[:].rearrange("p n j -> p (n j)"))
+        nc.vector.tensor_copy(k_bf[:, :, 2], k_win[2][:].indirect(offsets[:]))
+        halves = [slice(h * N // 2, (h + 1) * N // 2) for h in range(2)]
+        for h, cols in enumerate(halves):
+            nc.vector.tensor_copy(k_bf[:, cols, 3], k_win[3][:].indirect(offsets[:, h * N // 32 : (h + 1) * N // 32]))
+        for cols in halves:
+            nc.vector.quantize_mx(
+                k_codes[:, cols].bitcast(FP8X4), k_scales[:, cols], k_bf[:, cols, :].rearrange("p n j -> p (n j)")
+            )
 
         q_bf = keep.tile([P, NQ, PACK], BF16, name="q_bf", align_bytes=64)
         q_codes = keep.tile([P, NQ], U32, name="q_codes", align_bytes=64)

@@ -137,7 +137,7 @@ def tile_attend_mqa_topk_ks_kernel(tc, qT, kT, vT, ks, vs, offs, out):
                 )
 
         w_bf = keep.tile([P, NQ, PACK], BF16, name="w_bf", align_bytes=64)
-        early = keep.tile([P, 2 * P, PACK], BF16, name="early", align_bytes=64)
+        neg_m = keep.tile([P, QB], F32, name="neg_m", tag="early", align_bytes=64)
         late = [keep.tile([P, P, PACK], BF16, name=f"late{g}", align_bytes=64) for g in range(2)]
 
         def turn(row, bank, dst, col, copy):
@@ -147,19 +147,17 @@ def tile_attend_mqa_topk_ks_kernel(tc, qT, kT, vT, ks, vs, offs, out):
             pairs = dst[:].rearrange("s e t -> s (e t)").bitcast(F32).rearrange("s (e u) -> s e u", u=2)
             copy(pairs[:, col : col + P, :], bank[:, 0:2, :].rearrange("s u e -> s e u"))
 
-        def values(g):
-            v_row = keep.tile([P, N], BF16, name=f"v_row{g}")
+        def gather(g):
+            v_row = keep.tile([P, N], BF16, name=f"v_row{g}", tag=f"v_row{g}")
             nc.vector.tensor_copy(dealt(v_row[:]), v_win[g][:].indirect(offsets[:]))
-            if g < 2:
-                turn(v_row[:], v_bank[g % 2], early, g * P, nc.scalar.copy)
-            else:
-                turn(v_row[:], s_bank[g - 2], late[g - 2], 0, nc.scalar.copy if g == 2 else nc.vector.tensor_copy)
+            return v_row[:]
 
-        values(0)
+        def values(g):
+            turn(gather(g), s_bank[g - 2], late[g - 2], 0, nc.scalar.copy if g == 2 else nc.vector.tensor_copy)
 
-        neg_m = keep.tile([P, QB], F32, name="neg_m")
+        v_row0 = gather(0)
+
         total = keep.tile([P, QB], F32, name="total")
-        inv = keep.tile([P, QB], F32, name="inv")
         for b in range(QB):
             for c in range(SB):
                 nc.tensor.transpose(a_bank[b][:, c, :], a_t[b][:, c, :], ident[:])
@@ -172,17 +170,20 @@ def tile_attend_mqa_topk_ks_kernel(tc, qT, kT, vT, ks, vs, offs, out):
                 bias=neg_m[:, b : b + 1], scale=-1.0, accum_out=total[:, b : b + 1],
             )
             p_sb.append(p_b)
-        values(1)
+        early = keep.tile([P, 2 * P, PACK], BF16, name="early", tag="early", align_bytes=64)
+        turn(v_row0, v_bank[0], early, 0, nc.scalar.copy)
+        turn(gather(1), v_bank[1], early, P, nc.scalar.copy)
         for b in range(QB):
             w_row = keep.tile([P, N], BF16, name=f"w_row{b}")
             nc.gpsimd.tensor_tensor(w_row[:], p_sb[b][:], vs_all[:], MULT)
-            turn(w_row[:], v_bank[1], w_bf, b * P, nc.scalar.copy)
-        nc.vector.reciprocal(inv[:], total[:])
+            turn(w_row[:], (s_bank[2], v_bank[1])[b], w_bf, b * P, nc.scalar.copy)
         values(2)
         early_codes = keep.tile([P, 2 * P], U32, name="early_codes", tag="v_win2", align_bytes=64)
         early_scales = keep.tile([P, 2 * P], U8, name="early_scales", align_bytes=64)
         nc.vector.quantize_mx(early_codes[:].bitcast(FP8X4), early_scales[:], early[:].rearrange("s e t -> s (e t)"))
         values(3)
+        inv = keep.tile([P, QB], F32, name="inv", tag="v_row2")
+        nc.vector.reciprocal(inv[:], total[:])
         held = keep.tile([P, NQ + P], U32, name="held", tag="v_win3", align_bytes=64)
         w_codes = held[:, 0:NQ]
         w_scales = keep.tile([P, NQ], U8, name="w_scales", align_bytes=64)

@@ -176,13 +176,18 @@ def tile_attend_mqa_topk_ks_kernel(tc, qT, kT, vT, ks, vs, offs, out):
         for b in range(QB):
             w_row = keep.tile([P, N], BF16, name=f"w_row{b}")
             nc.gpsimd.tensor_tensor(w_row[:], p_sb[b][:], vs_all[:], MULT)
-            turn(w_row[:], (s_bank[2], v_bank[1])[b], w_bf, b * P, nc.scalar.copy)
+            for u in range(2):
+                nc.tensor.transpose(v_bank[1][:, 2 * b + u, :], w_row[:].bitcast(F32)[:, u * P : (u + 1) * P], ident[:])
+        nc.scalar.copy(
+            w_bf[:].rearrange("s e t -> s (e t)").bitcast(F32).rearrange("s (b q u) -> s b q u", b=QB, u=2),
+            v_bank[1][:].rearrange("s (b u) q -> s b q u", u=2),
+        )
         values(2)
         early_codes = keep.tile([P, 2 * P], U32, name="early_codes", tag="v_win2", align_bytes=64)
         early_scales = keep.tile([P, 2 * P], U8, name="early_scales", align_bytes=64)
         nc.vector.quantize_mx(early_codes[:].bitcast(FP8X4), early_scales[:], early[:].rearrange("s e t -> s (e t)"))
         values(3)
-        inv = keep.tile([P, QB], F32, name="inv", tag="v_row2")
+        inv = keep.tile([P, QB], F32, name="inv", tag="v_row3")
         nc.vector.reciprocal(inv[:], total[:])
         held = keep.tile([P, NQ + P], U32, name="held", tag="v_win3", align_bytes=64)
         w_codes = held[:, 0:NQ]

@@ -153,7 +153,7 @@ def tile_attend_mqa_topk_ks_kernel(tc, qT, kT, vT, ks, vs, offs, out):
             return v_row[:]
 
         def values(g):
-            turn(gather(g), s_bank[g - 2], late[g - 2], 0, nc.scalar.copy if g == 2 else nc.vector.tensor_copy)
+            turn(gather(g), s_bank[g - 2], late[g - 2], 0, nc.scalar.copy)
 
         v_row0 = gather(0)
 
@@ -212,13 +212,22 @@ def tile_attend_mqa_topk_ks_kernel(tc, qT, kT, vT, ks, vs, offs, out):
             product(s_bank[2 + b], b, early_codes[:], early_scales[:], 2 * P, y_sb[:], False)
             nc.sync.dma_start(out_q[:, b, 0 : 2 * P], y_sb[:])
 
+        codes2 = held[:, NQ:]
+        scales2 = keep.tile([P, P], U8, name="scales2", align_bytes=64)
+        nc.vector.quantize_mx(codes2.bitcast(FP8X4), scales2[:], late[0][:].rearrange("s e t -> s (e t)"))
         codes3 = keep.tile([P, P], U32, name="codes3", align_bytes=64)
-        for g, codes, banks in ((2, held[:, NQ:], a_bank), (3, codes3[:], s_bank)):
-            scales = keep.tile([P, P], U8, name=f"scales{g}", align_bytes=64)
-            nc.vector.quantize_mx(codes.bitcast(FP8X4), scales[:], late[g - 2][:].rearrange("s e t -> s (e t)"))
-            y_sb = keep.tile([P, QB, P], F32, name=f"y_late{g}")
-            e_cols = slice(g * P, (g + 1) * P)
-            for b in range(QB):
-                product(banks[b], b, codes, scales[:], P, y_sb[:, b, :], g == 3)
-            queue = nc.scalar if g == 2 else nc.sync
-            queue.dma_start(out_q[:, :, e_cols], y_sb[:])
+        scales3 = keep.tile([P, P], U8, name="scales3", align_bytes=64)
+        nc.vector.quantize_mx(codes3[:].bitcast(FP8X4), scales3[:], late[1][:].rearrange("s e t -> s (e t)"))
+        y2 = keep.tile([P, QB, P], F32, name="y2")
+        for b in range(QB):
+            cols = slice(b * P, (b + 1) * P)
+            nc.tensor.matmul_mx(
+                a_bank[0][:, b, :], w_codes[:, cols].bitcast(FP8X4), w_scales[:, cols],
+                codes2.bitcast(FP8X4), scales2[:], start=True, stop=True,
+            )
+        nc.vector.tensor_tensor(y2[:], a_bank[0][:, 0:QB, :], inv[:].unsqueeze(2).to_broadcast([P, QB, P]), MULT)
+        nc.sync.dma_start(out_q[:, :, 2 * P : 3 * P], y2[:])
+        for b, (bank, queue) in enumerate(((a_bank[1], nc.sync), (v_bank[0], nc.scalar))):
+            y3 = keep.tile([P, P], F32, name=f"y3_{b}")
+            product(bank, b, codes3[:], scales3[:], P, y3[:], b == 0)
+            queue.dma_start(out_q[:, b, 3 * P : 4 * P], y3[:])

@@ -55,10 +55,6 @@ def tile_attend_mqa_topk_ks_kernel(tc, qT, kT, vT, ks, vs, offs, out):
         for g in range(EB):
             nc.sync.dma_start(v_win[g][:], v_planes[g])
 
-        warm = keep.tile([P, 1], F32, name="warm")
-        nc.vector.memset(warm[:], 0.0)
-        nc.scalar.activation(warm[:], warm[:], ACT.Exp)
-
         ident = keep.tile([P, P], F32, name="ident")
         make_identity(nc, ident[:])
 

@@ -43,7 +43,7 @@ def tile_attend_mqa_topk_ks_kernel(tc, qT, kT, vT, ks, vs, offs, out):
 
         k_planes = kT.rearrange("(p j) n -> j p n", j=PACK)
         v_planes = vT.rearrange("(g e) n -> g e n", e=P)
-        for t, (win, row) in enumerate(((vs_win, vs), (ks_win, ks))):
+        for t, (win, row) in enumerate(((ks_win, ks), (vs_win, vs))):
             nc.sync.dma_start(k_win[t][:], k_planes[t])
             if t == 0:
                 nc.sync.dma_start(offsets[:], offs)
@@ -58,12 +58,10 @@ def tile_attend_mqa_topk_ks_kernel(tc, qT, kT, vT, ks, vs, offs, out):
         ident = keep.tile([P, P], F32, name="ident")
         make_identity(nc, ident[:])
 
-        s_bank = [psum.tile([P, PACK, P], F32, name=f"s_bank{i}") for i in range(4)]
-        a_bank = [psum.tile([P, PACK, P], F32, name=f"a_bank{i}") for i in range(2)]
-        v_bank = [psum.tile([P, PACK, P], F32, name=f"v_bank{i}") for i in range(2)]
+        bank = [psum.tile([P, PACK, P], F32, name=f"bank{i}") for i in range(8)]
 
-        def flat(bank, width):
-            return bank[:].rearrange("p c s -> p (c s)")[:, 0:width]
+        def flat(tile, width):
+            return tile[:].rearrange("p c s -> p (c s)")[:, 0:width]
 
         def dealt(row):
             return row.rearrange("p (u b x) -> p b u x", u=2, x=16)
@@ -79,36 +77,39 @@ def tile_attend_mqa_topk_ks_kernel(tc, qT, kT, vT, ks, vs, offs, out):
         vs_all = keep.tile([P, N], F32, name="vs_all")
         ks_row = keep.tile([P, N], F32, name="ks_row")
         nks_col = keep.tile([P, SB], F32, name="nks_col")
-        vs_col = keep.tile([P, PACK], F32, name="vs_col")
+        vs_col = keep.tile([P, SB], F32, name="vs_col")
+
+        nks_all = keep.tile([P, N], F32, name="nks_all")
+
+        def spread(row, partition, sign, col, turned, wide):
+            for c in range(SB):
+                nc.tensor.transpose(turned[:, c, :], row[:, c * P : (c + 1) * P], ident[:])
+            nc.scalar.activation(col[:], turned[:, :, partition], ACT.Copy, scale=sign)
+            for c in range(SB):
+                nc.tensor.transpose(wide[:, c, :], col[:, c : c + 1].to_broadcast([P, P]), ident[:])
 
         nc.vector.tensor_copy(k_pair[:, 0, :], k_win[0][:].indirect(offsets[:]))
-        nc.vector.tensor_copy(vs_row[:], vs_win[:].indirect(offsets[:]))
-        nc.vector.tensor_copy(k_pair[:, 1, :], k_win[1][:].indirect(offsets[:]))
         nc.vector.tensor_copy(ks_row[:], ks_win[:].indirect(offsets[:]))
-        for c in range(SB):
-            nc.tensor.transpose(a_bank[1][:, c, :], vs_row[:, c * P : (c + 1) * P], ident[:])
-        nc.scalar.copy(vs_col[:], a_bank[1][:, :, 0])
-        for c in range(SB):
-            nc.tensor.transpose(v_bank[1][:, c, :], vs_col[:, c : c + 1].to_broadcast([P, P]), ident[:])
-        nc.scalar.copy(dealt(vs_all[:]), in_order(flat(v_bank[1], N)))
+        nc.vector.tensor_copy(k_pair[:, 1, :], k_win[1][:].indirect(offsets[:]))
+        nc.vector.tensor_copy(vs_row[:], vs_win[:].indirect(offsets[:]))
+        spread(ks_row, 0, -1.0, nks_col, bank[2], bank[3])
+        nc.scalar.copy(nks_all[:], flat(bank[3], N))
         nc.scalar.copy(k_bf[:, :, 0:2], k_pair[:].rearrange("p j n -> p n j"))
-        for c in range(SB):
-            nc.tensor.transpose(a_bank[0][:, c, :], ks_row[:, c * P : (c + 1) * P], ident[:])
-        nc.scalar.activation(nks_col[:], a_bank[0][:, :, 64], ACT.Copy, scale=-1.0)
+        spread(vs_row, 64, 1.0, vs_col, bank[5], bank[7])
+        nc.scalar.copy(dealt(vs_all[:]), in_order(flat(bank[7], N)))
         nc.vector.tensor_copy(k_bf[:, :, 2], k_win[2][:].indirect(offsets[:]))
         halves = [slice(h * N // 2, (h + 1) * N // 2) for h in range(2)]
         for h, cols in enumerate(halves):
             nc.vector.tensor_copy(k_bf[:, cols, 3], k_win[3][:].indirect(offsets[:, h * N // 32 : (h + 1) * N // 32]))
-        for cols in halves:
-            nc.vector.quantize_mx(
-                k_codes[:, cols].bitcast(FP8X4), k_scales[:, cols], k_bf[:, cols, :].rearrange("p n j -> p (n j)")
-            )
 
         q_bf = keep.tile([P, NQ, PACK], BF16, name="q_bf", align_bytes=64)
         q_codes = keep.tile([P, NQ], U32, name="q_codes", align_bytes=64)
         q_scales = keep.tile([P, NQ], U8, name="q_scales", align_bytes=64)
-        for b in range(QB):
+        for b, cols in enumerate(halves):
             rows = slice(b * P, (b + 1) * P)
+            nc.vector.quantize_mx(
+                k_codes[:, cols].bitcast(FP8X4), k_scales[:, cols], k_bf[:, cols, :].rearrange("p n j -> p (n j)")
+            )
             nc.scalar.copy(
                 q_bf[:, rows, :].rearrange("p (c i) j -> p c j i", i=4),
                 q_raw[:, :, rows].rearrange("p j (c i) -> p c j i", i=4),
@@ -117,113 +118,115 @@ def tile_attend_mqa_topk_ks_kernel(tc, qT, kT, vT, ks, vs, offs, out):
                 q_codes[:, rows].bitcast(FP8X4), q_scales[:, rows], q_bf[:, rows, :].rearrange("p q j -> p (q j)")
             )
 
-        a_t = [keep.tile([P, SB, P], F32, name=f"a_t{b}") for b in range(QB)]
-        for b in range(QB):
-            rows = slice(b * P, (b + 1) * P)
-            for c in range(SB):
-                cols = slice(c * P, (c + 1) * P)
-                nc.tensor.matmul_mx(
-                    s_bank[2 * b + c // 2][:, c % 2, :], k_codes[:, cols].bitcast(FP8X4), k_scales[:, cols],
-                    q_codes[:, rows].bitcast(FP8X4), q_scales[:, rows], start=True, stop=True,
-                )
-        for b in range(QB):
-            for c in range(SB):
-                nc.scalar.activation(
-                    a_t[b][:, c, :], s_bank[2 * b + c // 2][:, c % 2, :], ACT.Copy, scale=nks_col[:, c : c + 1]
-                )
-
-        w_bf = keep.tile([P, NQ, PACK], BF16, name="w_bf", align_bytes=64)
-        neg_m = keep.tile([P, QB], F32, name="neg_m", tag="early", align_bytes=64)
-        late = [keep.tile([P, P, PACK], BF16, name=f"late{g}", align_bytes=64) for g in range(2)]
-
-        def turn(row, bank, dst, col, copy):
-            words = row.bitcast(F32)
-            for u in range(2):
-                nc.tensor.transpose(bank[:, u, :], words[:, u * P : (u + 1) * P], ident[:])
-            pairs = dst[:].rearrange("s e t -> s (e t)").bitcast(F32).rearrange("s (e u) -> s e u", u=2)
-            copy(pairs[:, col : col + P, :], bank[:, 0:2, :].rearrange("s u e -> s e u"))
+        neg_a0 = keep.tile([P, N], F32, name="neg_a0")
+        a_t = keep.tile([P, SB, P], F32, name="a_t")
+        for h, cols in enumerate(halves):
+            nc.tensor.matmul_mx(
+                flat(bank[h], N // 2), q_codes[:, 0:P].bitcast(FP8X4), q_scales[:, 0:P],
+                k_codes[:, cols].bitcast(FP8X4), k_scales[:, cols], start=True, stop=True,
+            )
+            nc.vector.tensor_tensor(neg_a0[:, cols], flat(bank[h], N // 2), nks_all[:, cols], MULT)
+        for c in range(SB):
+            cols = slice(c * P, (c + 1) * P)
+            nc.tensor.matmul_mx(
+                bank[2 + c // 2][:, c % 2, :], k_codes[:, cols].bitcast(FP8X4), k_scales[:, cols],
+                q_codes[:, P:NQ].bitcast(FP8X4), q_scales[:, P:NQ], start=True, stop=True,
+            )
+        for c in range(SB):
+            nc.scalar.activation(
+                a_t[:, c, :], bank[2 + c // 2][:, c % 2, :], ACT.Copy, scale=nks_col[:, c : c + 1]
+            )
 
         def gather(g):
             v_row = keep.tile([P, N], BF16, name=f"v_row{g}", tag=f"v_row{g}")
             nc.vector.tensor_copy(dealt(v_row[:]), v_win[g][:].indirect(offsets[:]))
             return v_row[:]
 
-        def values(g):
-            turn(gather(g), s_bank[g - 2], late[g - 2], 0, nc.scalar.copy)
+        def turn(row, turned, dst, col):
+            words = row.bitcast(F32)
+            for u in range(2):
+                nc.tensor.transpose(turned[:, u, :], words[:, u * P : (u + 1) * P], ident[:])
+            pairs = dst[:].rearrange("s e t -> s (e t)").bitcast(F32).rearrange("s (e u) -> s e u", u=2)
+            nc.scalar.copy(pairs[:, col : col + P, :], turned[:, 0:2, :].rearrange("s u e -> s e u"))
 
         v_row0 = gather(0)
-
+        neg_m = keep.tile([P, QB], F32, name="neg_m", tag="early", align_bytes=64)
         total = keep.tile([P, QB], F32, name="total")
-        for b in range(QB):
-            for c in range(SB):
-                nc.tensor.transpose(a_bank[b][:, c, :], a_t[b][:, c, :], ident[:])
+        for c in range(SB):
+            nc.tensor.transpose(bank[5][:, c, :], a_t[:, c, :], ident[:])
         p_sb = []
-        for b in range(QB):
-            nc.vector.tensor_reduce(neg_m[:, b : b + 1], flat(a_bank[b], N), AXIS_X, MIN)
+        for b, neg_a in enumerate((neg_a0[:], flat(bank[5], N))):
+            nc.vector.tensor_reduce(neg_m[:, b : b + 1], neg_a, AXIS_X, MIN)
             p_b = keep.tile([P, N], F32, name=f"p_sb{b}")
             nc.scalar.activation(
-                dealt(p_b[:]), in_order(flat(a_bank[b], N)), ACT.Exp,
+                dealt(p_b[:]), in_order(neg_a), ACT.Exp,
                 bias=neg_m[:, b : b + 1], scale=-1.0, accum_out=total[:, b : b + 1],
             )
             p_sb.append(p_b)
-        early = keep.tile([P, 2 * P, PACK], BF16, name="early", tag="early", align_bytes=64)
-        turn(v_row0, v_bank[0], early, 0, nc.scalar.copy)
-        turn(gather(1), v_bank[1], early, P, nc.scalar.copy)
-        for b in range(QB):
-            w_row = keep.tile([P, N], BF16, name=f"w_row{b}")
-            nc.gpsimd.tensor_tensor(w_row[:], p_sb[b][:], vs_all[:], MULT)
-            for u in range(2):
-                nc.tensor.transpose(v_bank[1][:, 2 * b + u, :], w_row[:].bitcast(F32)[:, u * P : (u + 1) * P], ident[:])
-        nc.scalar.copy(
-            w_bf[:].rearrange("s e t -> s (e t)").bitcast(F32).rearrange("s (b q u) -> s b q u", b=QB, u=2),
-            v_bank[1][:].rearrange("s (b u) q -> s b q u", u=2),
-        )
-        values(2)
-        early_codes = keep.tile([P, 2 * P], U32, name="early_codes", tag="v_win2", align_bytes=64)
-        early_scales = keep.tile([P, 2 * P], U8, name="early_scales", align_bytes=64)
-        nc.vector.quantize_mx(early_codes[:].bitcast(FP8X4), early_scales[:], early[:].rearrange("s e t -> s (e t)"))
-        values(3)
-        inv = keep.tile([P, QB], F32, name="inv", tag="v_row3")
-        nc.vector.reciprocal(inv[:], total[:])
-        held = keep.tile([P, NQ + P], U32, name="held", tag="v_win3", align_bytes=64)
-        w_codes = held[:, 0:NQ]
-        w_scales = keep.tile([P, NQ], U8, name="w_scales", align_bytes=64)
-        nc.vector.quantize_mx(w_codes.bitcast(FP8X4), w_scales[:], w_bf[:].rearrange("s e t -> s (e t)"))
 
-        def product(bank, b, v_codes, v_scales, width, y_sb, on_vector):
-            cols = slice(b * P, (b + 1) * P)
-            y = flat(bank, width)
-            nc.tensor.matmul_mx(
-                y, w_codes[:, cols].bitcast(FP8X4), w_scales[:, cols], v_codes.bitcast(FP8X4), v_scales,
-                start=True, stop=True,
+        w_bf = keep.tile([P, NQ, PACK], BF16, name="w_bf", align_bytes=64)
+        early = keep.tile([P, 2 * P, PACK], BF16, name="early", tag="early", align_bytes=64)
+        late = [keep.tile([P, P, PACK], BF16, name=f"late{g}", tag=f"late{g}", align_bytes=64) for g in range(2)]
+
+        w_row = [keep.tile([P, N], BF16, name=f"w_row{b}") for b in range(QB)]
+        for b in range(QB):
+            nc.gpsimd.tensor_tensor(w_row[b][:], p_sb[b][:], vs_all[:], MULT)
+        turn(v_row0, bank[6], early, 0)
+        turn(w_row[0][:], bank[0], w_bf, 0)
+        turn(gather(1), bank[7], early, P)
+        turn(w_row[1][:], bank[7], w_bf, P)
+        inv = keep.tile([P, QB], F32, name="inv", tag="v_win1", align_bytes=64)
+        nc.vector.reciprocal(inv[:], total[:])
+        turn(gather(2), bank[2], late[0], 0)
+
+        held = keep.tile([P, 3 * P], U32, name="held", tag="v_win2", align_bytes=64)
+        early_codes = held[:, 0 : 2 * P]
+        early_scales = keep.tile([P, 2 * P], U8, name="early_scales", align_bytes=64)
+        w_scales = [keep.tile([P, P], U8, name=f"w_scales{b}", align_bytes=64) for b in range(QB)]
+        w_codes = [held[:, 2 * P :]]
+
+        def quantize_w(b):
+            nc.vector.quantize_mx(
+                w_codes[b].bitcast(FP8X4), w_scales[b][:], w_bf[:, b * P : (b + 1) * P, :].rearrange("s e t -> s (e t)")
             )
-            if on_vector:
-                nc.vector.tensor_scalar(y_sb, y, inv[:, b : b + 1], None, MULT)
-            else:
-                nc.scalar.activation(y_sb, y, ACT.Copy, scale=inv[:, b : b + 1])
+
+        def product(y, b, v_codes, v_scales):
+            nc.tensor.matmul_mx(
+                y, w_codes[b].bitcast(FP8X4), w_scales[b][:], v_codes.bitcast(FP8X4), v_scales, start=True, stop=True
+            )
 
         out_q = out[0].rearrange("(b q) e -> q b e", q=P)
-        for b in range(QB):
+
+        def early_product(b):
             y_sb = keep.tile([P, 2 * P], F32, name=f"y_early{b}")
-            product(s_bank[2 + b], b, early_codes[:], early_scales[:], 2 * P, y_sb[:], False)
+            product(flat(bank[4 + b], 2 * P), b, early_codes, early_scales[:])
+            nc.scalar.activation(y_sb[:], flat(bank[4 + b], 2 * P), ACT.Copy, scale=inv[:, b : b + 1])
             nc.sync.dma_start(out_q[:, b, 0 : 2 * P], y_sb[:])
 
-        codes2 = held[:, NQ:]
+        quantize_w(0)
+        nc.vector.quantize_mx(early_codes.bitcast(FP8X4), early_scales[:], early[:].rearrange("s e t -> s (e t)"))
+        early_product(0)
+
+        turn(gather(3), bank[3], late[1], 0)
+        last = keep.tile([P, 2 * P], U32, name="last", tag="v_win3", align_bytes=64)
+        w_codes.append(last[:, 0:P])
+        codes2 = last[:, P:]
         scales2 = keep.tile([P, P], U8, name="scales2", align_bytes=64)
+        quantize_w(1)
         nc.vector.quantize_mx(codes2.bitcast(FP8X4), scales2[:], late[0][:].rearrange("s e t -> s (e t)"))
+        early_product(1)
+        y2 = keep.tile([P, QB, P], F32, name="y2", tag="late1", align_bytes=64)
+        for b in range(QB):
+            product(bank[6][:, b, :], b, codes2, scales2[:])
         codes3 = keep.tile([P, P], U32, name="codes3", align_bytes=64)
         scales3 = keep.tile([P, P], U8, name="scales3", align_bytes=64)
         nc.vector.quantize_mx(codes3[:].bitcast(FP8X4), scales3[:], late[1][:].rearrange("s e t -> s (e t)"))
-        y2 = keep.tile([P, QB, P], F32, name="y2")
-        for b in range(QB):
-            cols = slice(b * P, (b + 1) * P)
-            nc.tensor.matmul_mx(
-                a_bank[0][:, b, :], w_codes[:, cols].bitcast(FP8X4), w_scales[:, cols],
-                codes2.bitcast(FP8X4), scales2[:], start=True, stop=True,
-            )
-        nc.vector.tensor_tensor(y2[:], a_bank[0][:, 0:QB, :], inv[:].unsqueeze(2).to_broadcast([P, QB, P]), MULT)
+        nc.vector.tensor_tensor(y2[:], bank[6][:, 0:QB, :], inv[:].unsqueeze(2).to_broadcast([P, QB, P]), MULT)
         nc.sync.dma_start(out_q[:, :, 2 * P : 3 * P], y2[:])
-        for b, (bank, queue) in enumerate(((a_bank[1], nc.sync), (v_bank[0], nc.scalar))):
-            y3 = keep.tile([P, P], F32, name=f"y3_{b}")
-            product(bank, b, codes3[:], scales3[:], P, y3[:], b == 0)
-            queue.dma_start(out_q[:, b, 3 * P : 4 * P], y3[:])
+        y3 = [keep.tile([P, P], F32, name=f"y3_{b}") for b in range(QB)]
+        product(flat(bank[7], P), 0, codes3[:], scales3[:])
+        nc.vector.tensor_scalar(y3[0][:], flat(bank[7], P), inv[:, 0:1], None, MULT)
+        nc.sync.dma_start(out_q[:, 0, 3 * P : 4 * P], y3[0][:])
+        product(flat(bank[0], P), 1, codes3[:], scales3[:])
+        nc.scalar.activation(y3[1][:], flat(bank[0], P), ACT.Copy, scale=inv[:, 1:2])
+        nc.scalar.dma_start(out_q[:, 1, 3 * P : 4 * P], y3[1][:])

@@ -212,17 +212,18 @@ def tile_attend_mqa_topk_ks_kernel(tc, qT, kT, vT, ks, vs, offs, out):
         w_codes.append(last[:, 0:P])
         codes2 = last[:, P:]
         scales2 = keep.tile([P, P], U8, name="scales2", align_bytes=64)
-        quantize_w(1)
         nc.vector.quantize_mx(codes2.bitcast(FP8X4), scales2[:], late[0][:].rearrange("s e t -> s (e t)"))
+        quantize_w(1)
+        y2 = keep.tile([P, QB, P], F32, name="y2")
+        product(flat(bank[6], P), 0, codes2, scales2[:])
+        nc.vector.tensor_scalar(y2[:, 0, :], flat(bank[6], P), inv[:, 0:1], None, MULT)
+        product(flat(bank[1], P), 1, codes2, scales2[:])
+        nc.scalar.activation(y2[:, 1, :], flat(bank[1], P), ACT.Copy, scale=inv[:, 1:2])
+        nc.sync.dma_start(out_q[:, :, 2 * P : 3 * P], y2[:])
         early_product(1)
-        y2 = keep.tile([P, QB, P], F32, name="y2", tag="late1", align_bytes=64)
-        for b in range(QB):
-            product(bank[6][:, b, :], b, codes2, scales2[:])
         codes3 = keep.tile([P, P], U32, name="codes3", align_bytes=64)
         scales3 = keep.tile([P, P], U8, name="scales3", align_bytes=64)
         nc.vector.quantize_mx(codes3[:].bitcast(FP8X4), scales3[:], late[1][:].rearrange("s e t -> s (e t)"))
-        nc.vector.tensor_tensor(y2[:], bank[6][:, 0:QB, :], inv[:].unsqueeze(2).to_broadcast([P, QB, P]), MULT)
-        nc.sync.dma_start(out_q[:, :, 2 * P : 3 * P], y2[:])
         y3 = [keep.tile([P, P], F32, name=f"y3_{b}") for b in range(QB)]
         product(flat(bank[7], P), 0, codes3[:], scales3[:])
         nc.vector.tensor_scalar(y3[0][:], flat(bank[7], P), inv[:, 0:1], None, MULT)

@@ -149,18 +149,22 @@ def tile_attend_mqa_topk_ks_kernel(tc, qT, kT, vT, ks, vs, offs, out):
             pairs = dst[:].rearrange("s e t -> s (e t)").bitcast(F32).rearrange("s (e u) -> s e u", u=2)
             nc.scalar.copy(pairs[:, col : col + P, :], turned[:, 0:2, :].rearrange("s u e -> s e u"))
 
+        half_m = keep.tile([P, 2], F32, name="half_m")
+        for h, cols in enumerate(halves):
+            nc.vector.tensor_reduce(half_m[:, h : h + 1], neg_a0[:, cols], AXIS_X, MIN)
         v_row0 = gather(0)
-        neg_m = keep.tile([P, QB], F32, name="neg_m", tag="early", align_bytes=64)
+        neg_m = [keep.tile([P, 1], F32, name="neg_m0"), keep.tile([P, 1], F32, name="neg_m1", tag="early", align_bytes=64)]
         total = keep.tile([P, QB], F32, name="total")
         for c in range(SB):
             nc.tensor.transpose(bank[5][:, c, :], a_t[:, c, :], ident[:])
+        nc.gpsimd.tensor_scalar(neg_m[0][:], half_m[:, 0:1], half_m[:, 1:2], None, MIN)
+        nc.vector.tensor_reduce(neg_m[1][:], flat(bank[5], N), AXIS_X, MIN)
         p_sb = []
         for b, neg_a in enumerate((neg_a0[:], flat(bank[5], N))):
-            nc.vector.tensor_reduce(neg_m[:, b : b + 1], neg_a, AXIS_X, MIN)
             p_b = keep.tile([P, N], F32, name=f"p_sb{b}")
             nc.scalar.activation(
                 dealt(p_b[:]), in_order(neg_a), ACT.Exp,
-                bias=neg_m[:, b : b + 1], scale=-1.0, accum_out=total[:, b : b + 1],
+                bias=neg_m[b][:], scale=-1.0, accum_out=total[:, b : b + 1],
             )
             p_sb.append(p_b)
 

@@ -14,6 +14,7 @@ U8 = mybir.dt.uint8
 FP8X4 = mybir.dt.float8_e4m3fn_x4
 MULT = mybir.AluOpType.mult
 MIN = mybir.AluOpType.min
+POW = mybir.AluOpType.pow
 AXIS_X = mybir.AxisListType.X
 ACT = mybir.ActivationFunctionType
 
@@ -175,12 +176,14 @@ def tile_attend_mqa_topk_ks_kernel(tc, qT, kT, vT, ks, vs, offs, out):
         w_row = [keep.tile([P, N], BF16, name=f"w_row{b}") for b in range(QB)]
         for b in range(QB):
             nc.gpsimd.tensor_tensor(w_row[b][:], p_sb[b][:], vs_all[:], MULT)
+        minus_one = keep.tile([P, QB], F32, name="minus_one")
+        nc.gpsimd.memset(minus_one[:], -1.0)
+        inv = keep.tile([P, QB], F32, name="inv")
+        nc.gpsimd.tensor_tensor(inv[:], total[:], minus_one[:], POW)
         turn(v_row0, bank[6], early, 0)
         turn(w_row[0][:], bank[0], w_bf, 0)
         turn(gather(1), bank[7], early, P)
         turn(w_row[1][:], bank[7], w_bf, P)
-        inv = keep.tile([P, QB], F32, name="inv", tag="v_win1", align_bytes=64)
-        nc.vector.reciprocal(inv[:], total[:])
         turn(gather(2), bank[2], late[0], 0)
 
         held = keep.tile([P, 3 * P], U32, name="held", tag="v_win2", align_bytes=64)
@@ -220,7 +223,7 @@ def tile_attend_mqa_topk_ks_kernel(tc, qT, kT, vT, ks, vs, offs, out):
         quantize_w(1)
         y2 = keep.tile([P, QB, P], F32, name="y2")
         product(flat(bank[6], P), 0, codes2, scales2[:])
-        nc.vector.tensor_scalar(y2[:, 0, :], flat(bank[6], P), inv[:, 0:1], None, MULT)
+        nc.scalar.activation(y2[:, 0, :], flat(bank[6], P), ACT.Copy, scale=inv[:, 0:1])
         product(flat(bank[1], P), 1, codes2, scales2[:])
         nc.scalar.activation(y2[:, 1, :], flat(bank[1], P), ACT.Copy, scale=inv[:, 1:2])
         nc.sync.dma_start(out_q[:, :, 2 * P : 3 * P], y2[:])

@@ -170,7 +170,10 @@ def tile_attend_mqa_topk_ks_kernel(tc, qT, kT, vT, ks, vs, offs, out):
             p_sb.append(p_b)
 
         w_bf = keep.tile([P, NQ, PACK], BF16, name="w_bf", align_bytes=64)
-        early = keep.tile([P, 2 * P, PACK], BF16, name="early", tag="early", align_bytes=64)
+        early = [
+            keep.tile([P, P, PACK], BF16, name="early0", tag="early", align_bytes=64),
+            keep.tile([P, P, PACK], BF16, name="early1", align_bytes=64),
+        ]
         late = [keep.tile([P, P, PACK], BF16, name=f"late{g}", tag=f"late{g}", align_bytes=64) for g in range(2)]
 
         w_row = [keep.tile([P, N], BF16, name=f"w_row{b}") for b in range(QB)]
@@ -180,10 +183,9 @@ def tile_attend_mqa_topk_ks_kernel(tc, qT, kT, vT, ks, vs, offs, out):
         nc.gpsimd.memset(minus_one[:], -1.0)
         inv = keep.tile([P, QB], F32, name="inv")
         nc.gpsimd.tensor_tensor(inv[:], total[:], minus_one[:], POW)
-        turn(v_row0, bank[6], early, 0)
+        turn(v_row0, bank[6], early[0], 0)
         turn(w_row[0][:], bank[0], w_bf, 0)
-        turn(gather(1), bank[7], early, P)
-        turn(w_row[1][:], bank[7], w_bf, P)
+        turn(gather(1), bank[7], early[1], 0)
         turn(gather(2), bank[2], late[0], 0)
 
         held = keep.tile([P, 3 * P], U32, name="held", tag="v_win2", align_bytes=64)
@@ -210,9 +212,17 @@ def tile_attend_mqa_topk_ks_kernel(tc, qT, kT, vT, ks, vs, offs, out):
             nc.scalar.activation(y_sb[:], flat(bank[4 + b], 2 * P), ACT.Copy, scale=inv[:, b : b + 1])
             nc.sync.dma_start(out_q[:, b, 0 : 2 * P], y_sb[:])
 
+        def quantize_early(g):
+            cols = slice(g * P, (g + 1) * P)
+            nc.vector.quantize_mx(
+                early_codes[:, cols].bitcast(FP8X4), early_scales[:, cols], early[g][:].rearrange("s e t -> s (e t)")
+            )
+
+        quantize_early(0)
         quantize_w(0)
-        nc.vector.quantize_mx(early_codes.bitcast(FP8X4), early_scales[:], early[:].rearrange("s e t -> s (e t)"))
+        quantize_early(1)
         early_product(0)
+        turn(w_row[1][:], bank[2], w_bf, P)
 
         turn(gather(3), bank[3], late[1], 0)
         last = keep.tile([P, 2 * P], U32, name="last", tag="v_win3", align_bytes=64)

@@ -143,12 +143,18 @@ def tile_attend_mqa_topk_ks_kernel(tc, qT, kT, vT, ks, vs, offs, out):
             nc.vector.tensor_copy(dealt(v_row[:]), v_win[g][:].indirect(offsets[:]))
             return v_row[:]
 
-        def turn(row, turned, dst, col):
+        def transposes(row, turned):
             words = row.bitcast(F32)
             for u in range(2):
                 nc.tensor.transpose(turned[:, u, :], words[:, u * P : (u + 1) * P], ident[:])
+
+        def weave(turned, dst, col):
             pairs = dst[:].rearrange("s e t -> s (e t)").bitcast(F32).rearrange("s (e u) -> s e u", u=2)
-            nc.scalar.copy(pairs[:, col : col + P, :], turned[:, 0:2, :].rearrange("s u e -> s e u"))
+            nc.scalar.copy(pairs[:, col : col + P, :], turned.rearrange("s u e -> s e u"))
+
+        def turn(row, turned, dst, col):
+            transposes(row, turned[:, 0:2, :])
+            weave(turned[:, 0:2, :], dst, col)
 
         half_m = keep.tile([P, 2], F32, name="half_m")
         for h, cols in enumerate(halves):
@@ -186,7 +192,10 @@ def tile_attend_mqa_topk_ks_kernel(tc, qT, kT, vT, ks, vs, offs, out):
         turn(v_row0, bank[6], early[0], 0)
         turn(w_row[0][:], bank[0], w_bf, 0)
         turn(gather(1), bank[7], early[1], 0)
-        turn(gather(2), bank[2], late[0], 0)
+        transposes(gather(2), bank[2][:, 0:2, :])
+        transposes(w_row[1][:], bank[2][:, 2:4, :])
+        weave(bank[2][:, 0:2, :], late[0], 0)
+        weave(bank[2][:, 2:4, :], w_bf, P)
 
         held = keep.tile([P, 3 * P], U32, name="held", tag="v_win2", align_bytes=64)
         early_codes = held[:, 0 : 2 * P]
@@ -222,7 +231,6 @@ def tile_attend_mqa_topk_ks_kernel(tc, qT, kT, vT, ks, vs, offs, out):
         quantize_w(0)
         quantize_early(1)
         early_product(0)
-        turn(w_row[1][:], bank[2], w_bf, P)
 
         turn(gather(3), bank[3], late[1], 0)
         last = keep.tile([P, 2 * P], U32, name="last", tag="v_win3", align_bytes=64)

@@ -250,9 +250,9 @@ def tile_attend_mqa_topk_ks_kernel(tc, qT, kT, vT, ks, vs, offs, out):
         scales3 = keep.tile([P, P], U8, name="scales3", align_bytes=64)
         nc.vector.quantize_mx(codes3[:].bitcast(FP8X4), scales3[:], late[1][:].rearrange("s e t -> s (e t)"))
         y3 = [keep.tile([P, P], F32, name=f"y3_{b}") for b in range(QB)]
-        product(flat(bank[7], P), 0, codes3[:], scales3[:])
-        nc.vector.tensor_scalar(y3[0][:], flat(bank[7], P), inv[:, 0:1], None, MULT)
-        nc.sync.dma_start(out_q[:, 0, 3 * P : 4 * P], y3[0][:])
-        product(flat(bank[0], P), 1, codes3[:], scales3[:])
-        nc.scalar.activation(y3[1][:], flat(bank[0], P), ACT.Copy, scale=inv[:, 1:2])
-        nc.scalar.dma_start(out_q[:, 1, 3 * P : 4 * P], y3[1][:])
+        product(flat(bank[7], P), 1, codes3[:], scales3[:])
+        nc.vector.tensor_scalar(y3[1][:], flat(bank[7], P), inv[:, 1:2], None, MULT)
+        nc.sync.dma_start(out_q[:, 1, 3 * P : 4 * P], y3[1][:])
+        product(flat(bank[0], P), 0, codes3[:], scales3[:])
+        nc.scalar.activation(y3[0][:], flat(bank[0], P), ACT.Copy, scale=inv[:, 0:1])
+        nc.scalar.dma_start(out_q[:, 0, 3 * P : 4 * P], y3[0][:])

@@ -64,44 +64,38 @@ def tile_attend_mqa_topk_ks_kernel(tc, qT, kT, vT, ks, vs, offs, out):
         def flat(tile, width):
             return tile[:].rearrange("p c s -> p (c s)")[:, 0:width]
 
-        def dealt(row):
-            return row.rearrange("p (u b x) -> p b u x", u=2, x=16)
-
-        def in_order(row):
-            return row.rearrange("p (b u x) -> p b u x", u=2, x=16)
+        def by_place(row):
+            return row.rearrange("p (s t) -> p t s", t=PACK)
 
         k_bf = keep.tile([P, N, PACK], BF16, name="k_bf", align_bytes=64)
         k_codes = keep.tile([P, N], U32, name="k_codes", align_bytes=64)
         k_scales = keep.tile([P, N], U8, name="k_scales", align_bytes=64)
         k_pair = keep.tile([P, 2, N], F32, name="k_pair")
         vs_row = keep.tile([P, N], F32, name="vs_row")
-        vs_all = keep.tile([P, N], F32, name="vs_all")
         ks_row = keep.tile([P, N], F32, name="ks_row")
         nks_col = keep.tile([P, SB], F32, name="nks_col")
-        vs_col = keep.tile([P, SB], F32, name="vs_col")
-
-        nks_all = keep.tile([P, N], F32, name="nks_all")
-
-        def spread(row, partition, sign, col, turned, wide):
-            for c in range(SB):
-                nc.tensor.transpose(turned[:, c, :], row[:, c * P : (c + 1) * P], ident[:])
-            nc.scalar.activation(col[:], turned[:, :, partition], ACT.Copy, scale=sign)
-            for c in range(SB):
-                nc.tensor.transpose(wide[:, c, :], col[:, c : c + 1].to_broadcast([P, P]), ident[:])
+        vs_col = keep.tile([P, PACK], F32, name="vs_col")
+        nks_all = keep.tile([P, 2, PACK, N // 8], F32, name="nks_all")
 
         nc.vector.tensor_copy(k_pair[:, 0, :], k_win[0][:].indirect(offsets[:]))
         nc.vector.tensor_copy(ks_row[:], ks_win[:].indirect(offsets[:]))
         nc.vector.tensor_copy(k_pair[:, 1, :], k_win[1][:].indirect(offsets[:]))
         nc.vector.tensor_copy(vs_row[:], vs_win[:].indirect(offsets[:]))
-        spread(ks_row, 0, -1.0, nks_col, bank[2], bank[3])
-        nc.scalar.copy(nks_all[:], flat(bank[3], N))
+        for c in range(SB):
+            nc.tensor.transpose(bank[2][:, c, :], ks_row[:, c * P : (c + 1) * P], ident[:])
+        nc.scalar.activation(nks_col[:], bank[2][:, :, 0], ACT.Copy, scale=-1.0)
+        for c in range(SB):
+            nc.tensor.transpose(bank[3][:, c, :], nks_col[:, c : c + 1].to_broadcast([P, P]), ident[:])
+        nc.scalar.copy(nks_all[:], flat(bank[3], N).rearrange("p (h s t) -> p h t s", h=2, t=PACK))
         nc.scalar.copy(k_bf[:, :, 0:2], k_pair[:].rearrange("p j n -> p n j"))
-        spread(vs_row, 64, 1.0, vs_col, bank[5], bank[7])
-        nc.scalar.copy(dealt(vs_all[:]), in_order(flat(bank[7], N)))
+        for t in range(PACK):
+            nc.tensor.transpose(bank[5][:, t, :], vs_row[:, t::PACK], ident[:])
+        nc.scalar.copy(vs_col[:], bank[5][:, :, 64])
         nc.vector.tensor_copy(k_bf[:, :, 2], k_win[2][:].indirect(offsets[:]))
         halves = [slice(h * N // 2, (h + 1) * N // 2) for h in range(2)]
+        lists = [offsets[:, h * N // 32 : (h + 1) * N // 32] for h in range(2)]
         for h, cols in enumerate(halves):
-            nc.vector.tensor_copy(k_bf[:, cols, 3], k_win[3][:].indirect(offsets[:, h * N // 32 : (h + 1) * N // 32]))
+            nc.vector.tensor_copy(k_bf[:, cols, 3], k_win[3][:].indirect(lists[h]))
 
         q_bf = keep.tile([P, NQ, PACK], BF16, name="q_bf", align_bytes=64)
         q_codes = keep.tile([P, NQ], U32, name="q_codes", align_bytes=64)
@@ -119,139 +113,119 @@ def tile_attend_mqa_topk_ks_kernel(tc, qT, kT, vT, ks, vs, offs, out):
                 q_codes[:, rows].bitcast(FP8X4), q_scales[:, rows], q_bf[:, rows, :].rearrange("p q j -> p (q j)")
             )
 
-        neg_a0 = keep.tile([P, N], F32, name="neg_a0")
-        a_t = keep.tile([P, SB, P], F32, name="a_t")
-        for h, cols in enumerate(halves):
-            nc.tensor.matmul_mx(
-                flat(bank[h], N // 2), q_codes[:, 0:P].bitcast(FP8X4), q_scales[:, 0:P],
-                k_codes[:, cols].bitcast(FP8X4), k_scales[:, cols], start=True, stop=True,
-            )
-            nc.vector.tensor_tensor(neg_a0[:, cols], flat(bank[h], N // 2), nks_all[:, cols], MULT)
-        for c in range(SB):
-            cols = slice(c * P, (c + 1) * P)
-            nc.tensor.matmul_mx(
-                bank[2 + c // 2][:, c % 2, :], k_codes[:, cols].bitcast(FP8X4), k_scales[:, cols],
-                q_codes[:, P:NQ].bitcast(FP8X4), q_scales[:, P:NQ], start=True, stop=True,
-            )
-        for c in range(SB):
-            nc.scalar.activation(
-                a_t[:, c, :], bank[2 + c // 2][:, c % 2, :], ACT.Copy, scale=nks_col[:, c : c + 1]
-            )
+        neg_a = [keep.tile([P, 2, PACK, N // 8], F32, name=f"neg_a{b}") for b in range(QB)]
+        for b in range(QB):
+            rows = slice(b * P, (b + 1) * P)
+            for h, cols in enumerate(halves):
+                scores = flat(bank[2 * b + h], N // 2)
+                nc.tensor.matmul_mx(
+                    scores, q_codes[:, rows].bitcast(FP8X4), q_scales[:, rows],
+                    k_codes[:, cols].bitcast(FP8X4), k_scales[:, cols], start=True, stop=True,
+                )
+                nc.vector.tensor_tensor(neg_a[b][:, h, :, :], by_place(scores), nks_all[:, h, :, :], MULT)
 
-        def gather(g):
-            v_row = keep.tile([P, N], BF16, name=f"v_row{g}", tag=f"v_row{g}")
-            nc.vector.tensor_copy(dealt(v_row[:]), v_win[g][:].indirect(offsets[:]))
-            return v_row[:]
+        v_row = [keep.tile([P, N], BF16, name=f"v_row{g}") for g in range(EB)]
 
-        def transposes(row, turned):
-            words = row.bitcast(F32)
+        def gather_vector(g):
+            nc.vector.tensor_copy(v_row[g][:, halves[0]], v_win[g][:].indirect(lists[0]))
+
+        def gather_scalar(g):
+            nc.scalar.activation(v_row[g][:, halves[1]], v_win[g][:].indirect(lists[1]), ACT.Copy)
+
+        def turn_values(g, turned):
+            words = v_row[g][:].bitcast(F32)
             for u in range(2):
-                nc.tensor.transpose(turned[:, u, :], words[:, u * P : (u + 1) * P], ident[:])
+                nc.tensor.transpose(turned[:, u, :], words[:, u::2], ident[:])
 
-        def weave(turned, dst, col):
-            pairs = dst[:].rearrange("s e t -> s (e t)").bitcast(F32).rearrange("s (e u) -> s e u", u=2)
-            nc.scalar.copy(pairs[:, col : col + P, :], turned.rearrange("s u e -> s e u"))
+        def weave(turned, dst):
+            nc.scalar.copy(dst.rearrange("s (e u) -> s e u", u=2), turned[:, 0:2, :].rearrange("s u e -> s e u"))
 
-        def turn(row, turned, dst, col):
-            transposes(row, turned[:, 0:2, :])
-            weave(turned[:, 0:2, :], dst, col)
+        def quantize(codes, scales, words):
+            nc.vector.quantize_mx(codes.bitcast(FP8X4), scales, words.bitcast(BF16))
 
-        half_m = keep.tile([P, 2], F32, name="half_m")
-        for h, cols in enumerate(halves):
-            nc.vector.tensor_reduce(half_m[:, h : h + 1], neg_a0[:, cols], AXIS_X, MIN)
-        v_row0 = gather(0)
-        neg_m = [keep.tile([P, 1], F32, name="neg_m0"), keep.tile([P, 1], F32, name="neg_m1", tag="early", align_bytes=64)]
+        neg_m = [keep.tile([P, 1], F32, name=f"neg_m{b}") for b in range(QB)]
         total = keep.tile([P, QB], F32, name="total")
-        for c in range(SB):
-            nc.tensor.transpose(bank[5][:, c, :], a_t[:, c, :], ident[:])
-        nc.gpsimd.tensor_scalar(neg_m[0][:], half_m[:, 0:1], half_m[:, 1:2], None, MIN)
-        nc.vector.tensor_reduce(neg_m[1][:], flat(bank[5], N), AXIS_X, MIN)
-        p_sb = []
-        for b, neg_a in enumerate((neg_a0[:], flat(bank[5], N))):
-            p_b = keep.tile([P, N], F32, name=f"p_sb{b}")
+        p_sb = [keep.tile([P, PACK, P], F32, name=f"p_sb{b}") for b in range(QB)]
+        w_bf = [keep.tile([P, P, PACK], BF16, name=f"w_bf{b}", align_bytes=64) for b in range(QB)]
+        w_codes = [keep.tile([P, P], U32, name=f"w_codes{b}", align_bytes=64) for b in range(QB)]
+        w_scales = [keep.tile([P, P], U8, name=f"w_scales{b}", align_bytes=64) for b in range(QB)]
+
+        def weights(b, turned):
+            for t in range(PACK):
+                nc.tensor.transpose(turned[:, t, :], p_sb[b][:, t, :], ident[:])
+            nc.vector.tensor_tensor(
+                w_bf[b][:], turned[:].rearrange("s t q -> s q t"),
+                vs_col[:].unsqueeze(1).to_broadcast([P, P, PACK]), MULT,
+            )
+
+        def quantize_w(b):
+            nc.vector.quantize_mx(w_codes[b][:].bitcast(FP8X4), w_scales[b][:], w_bf[b][:].rearrange("s q t -> s (q t)"))
+
+        nc.scalar.activation(v_row[0][:], v_win[0][:].indirect(offsets[:]), ACT.Copy)
+        for b in range(QB):
+            nc.vector.tensor_reduce(neg_m[b][:], neg_a[b][:].rearrange("p h t s -> p (h t s)"), AXIS_X, MIN)
             nc.scalar.activation(
-                dealt(p_b[:]), in_order(neg_a), ACT.Exp,
+                p_sb[b][:].rearrange("p t (h s) -> p h t s", h=2), neg_a[b][:], ACT.Exp,
                 bias=neg_m[b][:], scale=-1.0, accum_out=total[:, b : b + 1],
             )
-            p_sb.append(p_b)
-
-        w_bf = keep.tile([P, NQ, PACK], BF16, name="w_bf", align_bytes=64)
-        early = [
-            keep.tile([P, P, PACK], BF16, name="early0", tag="early", align_bytes=64),
-            keep.tile([P, P, PACK], BF16, name="early1", align_bytes=64),
-        ]
-        late = [keep.tile([P, P, PACK], BF16, name=f"late{g}", tag=f"late{g}", align_bytes=64) for g in range(2)]
-
-        w_row = [keep.tile([P, N], BF16, name=f"w_row{b}") for b in range(QB)]
-        for b in range(QB):
-            nc.gpsimd.tensor_tensor(w_row[b][:], p_sb[b][:], vs_all[:], MULT)
         minus_one = keep.tile([P, QB], F32, name="minus_one")
         nc.gpsimd.memset(minus_one[:], -1.0)
         inv = keep.tile([P, QB], F32, name="inv")
         nc.gpsimd.tensor_tensor(inv[:], total[:], minus_one[:], POW)
-        turn(v_row0, bank[6], early[0], 0)
-        turn(w_row[0][:], bank[0], w_bf, 0)
-        turn(gather(1), bank[7], early[1], 0)
-        transposes(gather(2), bank[2][:, 0:2, :])
-        transposes(w_row[1][:], bank[2][:, 2:4, :])
-        weave(bank[2][:, 0:2, :], late[0], 0)
-        weave(bank[2][:, 2:4, :], w_bf, P)
 
-        held = keep.tile([P, 3 * P], U32, name="held", tag="v_win2", align_bytes=64)
-        early_codes = held[:, 0 : 2 * P]
+        early = [keep.tile([P, 2 * P], F32, name=f"early{g}", align_bytes=64) for g in range(2)]
+        early_codes = keep.tile([P, 2 * P], U32, name="early_codes", align_bytes=64)
         early_scales = keep.tile([P, 2 * P], U8, name="early_scales", align_bytes=64)
-        w_scales = [keep.tile([P, P], U8, name=f"w_scales{b}", align_bytes=64) for b in range(QB)]
-        w_codes = [held[:, 2 * P :]]
-
-        def quantize_w(b):
-            nc.vector.quantize_mx(
-                w_codes[b].bitcast(FP8X4), w_scales[b][:], w_bf[:, b * P : (b + 1) * P, :].rearrange("s e t -> s (e t)")
-            )
+        turn_values(0, bank[7])
+        gather_vector(1)
+        weights(0, bank[5])
+        weave(bank[7], early[0][:])
+        gather_scalar(1)
+        weights(1, bank[6])
+        quantize_w(0)
+        turn_values(1, bank[0])
+        weave(bank[0], early[1][:])
+        quantize(early_codes[:, 0:P], early_scales[:, 0:P], early[0][:])
+        quantize_w(1)
+        gather_vector(2)
+        gather_scalar(2)
+        quantize(early_codes[:, P:], early_scales[:, P:], early[1][:])
 
         def product(y, b, v_codes, v_scales):
             nc.tensor.matmul_mx(
-                y, w_codes[b].bitcast(FP8X4), w_scales[b][:], v_codes.bitcast(FP8X4), v_scales, start=True, stop=True
+                y, w_codes[b][:].bitcast(FP8X4), w_scales[b][:], v_codes.bitcast(FP8X4), v_scales, start=True, stop=True
             )
 
         out_q = out[0].rearrange("(b q) e -> q b e", q=P)
+        turn_values(2, bank[1])
+        for b in range(QB):
+            product(flat(bank[2 + b], 2 * P), b, early_codes[:], early_scales[:])
 
-        def early_product(b):
-            y_sb = keep.tile([P, 2 * P], F32, name=f"y_early{b}")
-            product(flat(bank[4 + b], 2 * P), b, early_codes, early_scales[:])
-            nc.scalar.activation(y_sb[:], flat(bank[4 + b], 2 * P), ACT.Copy, scale=inv[:, b : b + 1])
-            nc.sync.dma_start(out_q[:, b, 0 : 2 * P], y_sb[:])
-
-        def quantize_early(g):
-            cols = slice(g * P, (g + 1) * P)
-            nc.vector.quantize_mx(
-                early_codes[:, cols].bitcast(FP8X4), early_scales[:, cols], early[g][:].rearrange("s e t -> s (e t)")
-            )
-
-        quantize_early(0)
-        quantize_w(0)
-        quantize_early(1)
-        early_product(0)
-
-        turn(gather(3), bank[3], late[1], 0)
-        last = keep.tile([P, 2 * P], U32, name="last", tag="v_win3", align_bytes=64)
-        w_codes.append(last[:, 0:P])
-        codes2 = last[:, P:]
+        gather_vector(3)
+        gather_scalar(3)
+        turn_values(3, bank[7])
+        behind = keep.tile([P, 6 * P], F32, name="behind", tag="v_win3", align_bytes=64)
+        weave(bank[1], behind[:, 0 : 2 * P])
+        for b in range(QB):
+            y_early = behind[:, (2 + 2 * b) * P : (4 + 2 * b) * P]
+            nc.vector.tensor_scalar(y_early, flat(bank[2 + b], 2 * P), inv[:, b : b + 1], None, MULT)
+            nc.sync.dma_start(out_q[:, b, 0 : 2 * P], y_early)
+        codes2 = keep.tile([P, P], U32, name="codes2", align_bytes=64)
         scales2 = keep.tile([P, P], U8, name="scales2", align_bytes=64)
-        nc.vector.quantize_mx(codes2.bitcast(FP8X4), scales2[:], late[0][:].rearrange("s e t -> s (e t)"))
-        quantize_w(1)
+        quantize(codes2[:], scales2[:], behind[:, 0 : 2 * P])
+        last = keep.tile([P, 2 * P], F32, name="last", align_bytes=64)
+        weave(bank[7], last[:])
         y2 = keep.tile([P, QB, P], F32, name="y2")
-        product(flat(bank[6], P), 0, codes2, scales2[:])
-        nc.scalar.activation(y2[:, 0, :], flat(bank[6], P), ACT.Copy, scale=inv[:, 0:1])
-        product(flat(bank[1], P), 1, codes2, scales2[:])
-        nc.scalar.activation(y2[:, 1, :], flat(bank[1], P), ACT.Copy, scale=inv[:, 1:2])
+        for b in range(QB):
+            product(flat(bank[4 + b], P), b, codes2[:], scales2[:])
+            nc.scalar.activation(y2[:, b, :], flat(bank[4 + b], P), ACT.Copy, scale=inv[:, b : b + 1])
         nc.sync.dma_start(out_q[:, :, 2 * P : 3 * P], y2[:])
-        early_product(1)
         codes3 = keep.tile([P, P], U32, name="codes3", align_bytes=64)
         scales3 = keep.tile([P, P], U8, name="scales3", align_bytes=64)
-        nc.vector.quantize_mx(codes3[:].bitcast(FP8X4), scales3[:], late[1][:].rearrange("s e t -> s (e t)"))
+        quantize(codes3[:], scales3[:], last[:])
         y3 = [keep.tile([P, P], F32, name=f"y3_{b}") for b in range(QB)]
-        product(flat(bank[7], P), 1, codes3[:], scales3[:])
-        nc.vector.tensor_scalar(y3[1][:], flat(bank[7], P), inv[:, 1:2], None, MULT)
+        product(flat(bank[6], P), 1, codes3[:], scales3[:])
+        nc.vector.tensor_scalar(y3[1][:], flat(bank[6], P), inv[:, 1:2], None, MULT)
         nc.sync.dma_start(out_q[:, 1, 3 * P : 4 * P], y3[1][:])
         product(flat(bank[0], P), 0, codes3[:], scales3[:])
         nc.scalar.activation(y3[0][:], flat(bank[0], P), ACT.Copy, scale=inv[:, 0:1])

@@ -77,7 +77,7 @@ def tile_attend_mqa_topk_ks_kernel(tc, qT, kT, vT, ks, vs, offs, out):
         vs_col = keep.tile([P, PACK], F32, name="vs_col")
         nks_all = keep.tile([P, 2, PACK, N // 8], F32, name="nks_all")
 
-        nc.vector.tensor_copy(k_pair[:, 0, :], k_win[0][:].indirect(offsets[:]))
+        nc.scalar.activation(k_pair[:, 0, :], k_win[0][:].indirect(offsets[:]), ACT.Copy)
         nc.vector.tensor_copy(ks_row[:], ks_win[:].indirect(offsets[:]))
         nc.vector.tensor_copy(k_pair[:, 1, :], k_win[1][:].indirect(offsets[:]))
         nc.vector.tensor_copy(vs_row[:], vs_win[:].indirect(offsets[:]))
@@ -99,7 +99,7 @@ def tile_attend_mqa_topk_ks_kernel(tc, qT, kT, vT, ks, vs, offs, out):
 
         q_bf = keep.tile([P, NQ, PACK], BF16, name="q_bf", align_bytes=64)
         q_codes = keep.tile([P, NQ], U32, name="q_codes", align_bytes=64)
-        q_scales = keep.tile([P, NQ], U8, name="q_scales", align_bytes=64)
+        q_scales = keep.tile([P, NQ], U8, name="q_scales", tag="q_scales", align_bytes=64)
         for b, cols in enumerate(halves):
             rows = slice(b * P, (b + 1) * P)
             nc.vector.quantize_mx(
@@ -126,11 +126,11 @@ def tile_attend_mqa_topk_ks_kernel(tc, qT, kT, vT, ks, vs, offs, out):
 
         v_row = [keep.tile([P, N], BF16, name=f"v_row{g}") for g in range(EB)]
 
-        def gather_vector(g):
-            nc.vector.tensor_copy(v_row[g][:, halves[0]], v_win[g][:].indirect(lists[0]))
-
-        def gather_scalar(g):
-            nc.scalar.activation(v_row[g][:, halves[1]], v_win[g][:].indirect(lists[1]), ACT.Copy)
+        def gather_shared(g, scalar_slots):
+            nc.scalar.activation(
+                v_row[g][:, 0:scalar_slots], v_win[g][:].indirect(offsets[:, 0 : scalar_slots // 16]), ACT.Copy
+            )
+            nc.vector.tensor_copy(v_row[g][:, scalar_slots:], v_win[g][:].indirect(offsets[:, scalar_slots // 16 :]))
 
         def turn_values(g, turned):
             words = v_row[g][:].bitcast(F32)
@@ -143,14 +143,17 @@ def tile_attend_mqa_topk_ks_kernel(tc, qT, kT, vT, ks, vs, offs, out):
         def quantize(codes, scales, words):
             nc.vector.quantize_mx(codes.bitcast(FP8X4), scales, words.bitcast(BF16))
 
-        neg_m = [keep.tile([P, 1], F32, name=f"neg_m{b}") for b in range(QB)]
+        neg_m = [
+            keep.tile([P, 1], F32, name="neg_m0", tag="q_scales", align_bytes=64),
+            keep.tile([P, 1], F32, name="neg_m1", tag="early0", align_bytes=64),
+        ]
         total = keep.tile([P, QB], F32, name="total")
         p_sb = [keep.tile([P, PACK, P], F32, name=f"p_sb{b}") for b in range(QB)]
-        w_bf = [keep.tile([P, P, PACK], BF16, name=f"w_bf{b}", align_bytes=64) for b in range(QB)]
-        w_codes = [keep.tile([P, P], U32, name=f"w_codes{b}", align_bytes=64) for b in range(QB)]
+        w_bf = []
         w_scales = [keep.tile([P, P], U8, name=f"w_scales{b}", align_bytes=64) for b in range(QB)]
 
-        def weights(b, turned):
+        def weights(b, turned, tag):
+            w_bf.append(keep.tile([P, P, PACK], BF16, name=f"w_bf{b}", tag=tag, align_bytes=64))
             for t in range(PACK):
                 nc.tensor.transpose(turned[:, t, :], p_sb[b][:, t, :], ident[:])
             nc.vector.tensor_tensor(
@@ -159,7 +162,7 @@ def tile_attend_mqa_topk_ks_kernel(tc, qT, kT, vT, ks, vs, offs, out):
             )
 
         def quantize_w(b):
-            nc.vector.quantize_mx(w_codes[b][:].bitcast(FP8X4), w_scales[b][:], w_bf[b][:].rearrange("s q t -> s (q t)"))
+            nc.vector.quantize_mx(w_codes[b].bitcast(FP8X4), w_scales[b][:], w_bf[b][:].rearrange("s q t -> s (q t)"))
 
         nc.scalar.activation(v_row[0][:], v_win[0][:].indirect(offsets[:]), ACT.Copy)
         for b in range(QB):
@@ -173,36 +176,36 @@ def tile_attend_mqa_topk_ks_kernel(tc, qT, kT, vT, ks, vs, offs, out):
         inv = keep.tile([P, QB], F32, name="inv")
         nc.gpsimd.tensor_tensor(inv[:], total[:], minus_one[:], POW)
 
-        early = [keep.tile([P, 2 * P], F32, name=f"early{g}", align_bytes=64) for g in range(2)]
-        early_codes = keep.tile([P, 2 * P], U32, name="early_codes", align_bytes=64)
+        early0 = keep.tile([P, 2 * P], F32, name="early0", tag="early0", align_bytes=64)
         early_scales = keep.tile([P, 2 * P], U8, name="early_scales", align_bytes=64)
         turn_values(0, bank[7])
-        gather_vector(1)
-        weights(0, bank[5])
-        weave(bank[7], early[0][:])
-        gather_scalar(1)
-        weights(1, bank[6])
-        quantize_w(0)
+        nc.vector.tensor_copy(v_row[1][:], v_win[1][:].indirect(offsets[:]))
+        weights(0, bank[5], "v_win1")
+        weave(bank[7], early0[:])
+        weights(1, bank[6], "w_bf1")
         turn_values(1, bank[0])
-        weave(bank[0], early[1][:])
-        quantize(early_codes[:, 0:P], early_scales[:, 0:P], early[0][:])
+        early1 = keep.tile([P, 2 * P], F32, name="early1", align_bytes=64)
+        weave(bank[0], early1[:])
+        codes = keep.tile([P, 4 * P], U32, name="codes", align_bytes=64)
+        early_codes = codes[:, 0 : 2 * P]
+        w_codes = [codes[:, (2 + b) * P : (3 + b) * P] for b in range(QB)]
+        quantize(early_codes[:, 0:P], early_scales[:, 0:P], early0[:])
+        quantize_w(0)
         quantize_w(1)
-        gather_vector(2)
-        gather_scalar(2)
-        quantize(early_codes[:, P:], early_scales[:, P:], early[1][:])
+        quantize(early_codes[:, P:], early_scales[:, P:], early1[:])
+        gather_shared(2, 320)
 
         def product(y, b, v_codes, v_scales):
             nc.tensor.matmul_mx(
-                y, w_codes[b][:].bitcast(FP8X4), w_scales[b][:], v_codes.bitcast(FP8X4), v_scales, start=True, stop=True
+                y, w_codes[b].bitcast(FP8X4), w_scales[b][:], v_codes.bitcast(FP8X4), v_scales, start=True, stop=True
             )
 
         out_q = out[0].rearrange("(b q) e -> q b e", q=P)
         turn_values(2, bank[1])
         for b in range(QB):
-            product(flat(bank[2 + b], 2 * P), b, early_codes[:], early_scales[:])
+            product(flat(bank[2 + b], 2 * P), b, early_codes, early_scales[:])
 
-        gather_vector(3)
-        gather_scalar(3)
+        gather_shared(3, 256)
         turn_values(3, bank[7])
         behind = keep.tile([P, 6 * P], F32, name="behind", tag="v_win3", align_bytes=64)
         weave(bank[1], behind[:, 0 : 2 * P])

@@ -205,7 +205,7 @@ def tile_attend_mqa_topk_ks_kernel(tc, qT, kT, vT, ks, vs, offs, out):
         for b in range(QB):
             product(flat(bank[2 + b], 2 * P), b, early_codes, early_scales[:])
 
-        gather_shared(3, 256)
+        gather_shared(3, 192)
         turn_values(3, bank[7])
         behind = keep.tile([P, 6 * P], F32, name="behind", tag="v_win3", align_bytes=64)
         weave(bank[1], behind[:, 0 : 2 * P])

@@ -124,7 +124,7 @@ def tile_attend_mqa_topk_ks_kernel(tc, qT, kT, vT, ks, vs, offs, out):
                 )
                 nc.vector.tensor_tensor(neg_a[b][:, h, :, :], by_place(scores), nks_all[:, h, :, :], MULT)
 
-        v_row = [keep.tile([P, N], BF16, name=f"v_row{g}") for g in range(EB)]
+        v_row = [keep.tile([P, N], BF16, name=f"v_row{g}", tag=f"v_row{g}") for g in range(EB)]
 
         def gather_shared(g, scalar_slots):
             nc.scalar.activation(
@@ -207,25 +207,27 @@ def tile_attend_mqa_topk_ks_kernel(tc, qT, kT, vT, ks, vs, offs, out):
 
         gather_shared(3, 192)
         turn_values(3, bank[7])
-        behind = keep.tile([P, 6 * P], F32, name="behind", tag="v_win3", align_bytes=64)
+        behind = keep.tile([P, 4 * P], F32, name="behind", tag="v_win3", align_bytes=64)
         weave(bank[1], behind[:, 0 : 2 * P])
-        for b in range(QB):
-            y_early = behind[:, (2 + 2 * b) * P : (4 + 2 * b) * P]
-            nc.vector.tensor_scalar(y_early, flat(bank[2 + b], 2 * P), inv[:, b : b + 1], None, MULT)
-            nc.sync.dma_start(out_q[:, b, 0 : 2 * P], y_early)
+        nc.vector.tensor_scalar(behind[:, 2 * P :], flat(bank[3], 2 * P), inv[:, 1:2], None, MULT)
+        nc.sync.dma_start(out_q[:, 1, 0 : 2 * P], behind[:, 2 * P :])
         codes2 = keep.tile([P, P], U32, name="codes2", align_bytes=64)
         scales2 = keep.tile([P, P], U8, name="scales2", align_bytes=64)
         quantize(codes2[:], scales2[:], behind[:, 0 : 2 * P])
         last = keep.tile([P, 2 * P], F32, name="last", align_bytes=64)
         weave(bank[7], last[:])
+        y_early0 = keep.tile([P, 2 * P], F32, name="y_early0", tag="v_row3")
+        nc.scalar.activation(y_early0[:], flat(bank[2], 2 * P), ACT.Copy, scale=inv[:, 0:1])
+        nc.sync.dma_start(out_q[:, 0, 0 : 2 * P], y_early0[:])
         y2 = keep.tile([P, QB, P], F32, name="y2")
         for b in range(QB):
             product(flat(bank[4 + b], P), b, codes2[:], scales2[:])
-            nc.scalar.activation(y2[:, b, :], flat(bank[4 + b], P), ACT.Copy, scale=inv[:, b : b + 1])
-        nc.sync.dma_start(out_q[:, :, 2 * P : 3 * P], y2[:])
+        nc.scalar.activation(y2[:, 0, :], flat(bank[4], P), ACT.Copy, scale=inv[:, 0:1])
         codes3 = keep.tile([P, P], U32, name="codes3", align_bytes=64)
         scales3 = keep.tile([P, P], U8, name="scales3", align_bytes=64)
         quantize(codes3[:], scales3[:], last[:])
+        nc.vector.tensor_scalar(y2[:, 1, :], flat(bank[5], P), inv[:, 1:2], None, MULT)
+        nc.sync.dma_start(out_q[:, :, 2 * P : 3 * P], y2[:])
         y3 = [keep.tile([P, P], F32, name=f"y3_{b}") for b in range(QB)]
         product(flat(bank[6], P), 1, codes3[:], scales3[:])
         nc.vector.tensor_scalar(y3[1][:], flat(bank[6], P), inv[:, 1:2], None, MULT)

@@ -27,6 +27,7 @@ DV = 512
 QB = NQ // P
 EB = DV // P
 SB = N // P
+DMA_ALIGN = 256
 
 
 def tile_attend_mqa_topk_ks_kernel(tc, qT, kT, vT, ks, vs, offs, out):
@@ -36,11 +37,11 @@ def tile_attend_mqa_topk_ks_kernel(tc, qT, kT, vT, ks, vs, offs, out):
         psum = ctx.enter_context(tc.psum_pool(name="psum", bufs=1))
 
         offsets = keep.tile([P, N // 16], U16, name="offsets")
-        q_raw = keep.tile([P, PACK, NQ], F32, name="q_raw")
-        k_win = [keep.tile([P, T], F32, name=f"k_win{t}") for t in range(PACK)]
-        v_win = [keep.tile([P, T], F32, name=f"v_win{g}", tag=f"v_win{g}", align_bytes=64) for g in range(EB)]
-        ks_win = keep.tile([P, T], F32, name="ks_win")
-        vs_win = keep.tile([P, T], F32, name="vs_win")
+        q_raw = keep.tile([P, PACK, NQ], F32, name="q_raw", align_bytes=DMA_ALIGN)
+        k_win = [keep.tile([P, T], F32, name=f"k_win{t}", align_bytes=DMA_ALIGN) for t in range(PACK)]
+        v_win = [keep.tile([P, T], F32, name=f"v_win{g}", tag=f"v_win{g}", align_bytes=DMA_ALIGN) for g in range(EB)]
+        ks_win = keep.tile([P, T], F32, name="ks_win", align_bytes=DMA_ALIGN)
+        vs_win = keep.tile([P, T], F32, name="vs_win", align_bytes=DMA_ALIGN)
 
         k_planes = kT.rearrange("(p j) n -> j p n", j=PACK)
         v_planes = vT.rearrange("(g e) n -> g e n", e=P)
@@ -124,7 +125,7 @@ def tile_attend_mqa_topk_ks_kernel(tc, qT, kT, vT, ks, vs, offs, out):
                 )
                 nc.vector.tensor_tensor(neg_a[b][:, h, :, :], by_place(scores), nks_all[:, h, :, :], MULT)
 
-        v_row = [keep.tile([P, N], BF16, name=f"v_row{g}", tag=f"v_row{g}") for g in range(EB)]
+        v_row = [keep.tile([P, N], BF16, name=f"v_row{g}", tag=f"v_row{g}", align_bytes=DMA_ALIGN) for g in range(EB)]
 
         def gather_shared(g, scalar_slots):
             nc.scalar.activation(
@@ -153,7 +154,7 @@ def tile_attend_mqa_topk_ks_kernel(tc, qT, kT, vT, ks, vs, offs, out):
         w_scales = [keep.tile([P, P], U8, name=f"w_scales{b}", align_bytes=64) for b in range(QB)]
 
         def weights(b, turned, tag):
-            w_bf.append(keep.tile([P, P, PACK], BF16, name=f"w_bf{b}", tag=tag, align_bytes=64))
+            w_bf.append(keep.tile([P, P, PACK], BF16, name=f"w_bf{b}", tag=tag, align_bytes=DMA_ALIGN))
             for t in range(PACK):
                 nc.tensor.transpose(turned[:, t, :], p_sb[b][:, t, :], ident[:])
             nc.vector.tensor_tensor(
@@ -207,7 +208,7 @@ def tile_attend_mqa_topk_ks_kernel(tc, qT, kT, vT, ks, vs, offs, out):
 
         gather_shared(3, 192)
         turn_values(3, bank[7])
-        behind = keep.tile([P, 4 * P], F32, name="behind", tag="v_win3", align_bytes=64)
+        behind = keep.tile([P, 4 * P], F32, name="behind", tag="v_win3", align_bytes=DMA_ALIGN)
         weave(bank[1], behind[:, 0 : 2 * P])
         nc.vector.tensor_scalar(behind[:, 2 * P :], flat(bank[3], 2 * P), inv[:, 1:2], None, MULT)
         nc.sync.dma_start(out_q[:, 1, 0 : 2 * P], behind[:, 2 * P :])
@@ -216,10 +217,10 @@ def tile_attend_mqa_topk_ks_kernel(tc, qT, kT, vT, ks, vs, offs, out):
         quantize(codes2[:], scales2[:], behind[:, 0 : 2 * P])
         last = keep.tile([P, 2 * P], F32, name="last", align_bytes=64)
         weave(bank[7], last[:])
-        y_early0 = keep.tile([P, 2 * P], F32, name="y_early0", tag="v_row3")
+        y_early0 = keep.tile([P, 2 * P], F32, name="y_early0", tag="v_row3", align_bytes=DMA_ALIGN)
         nc.scalar.activation(y_early0[:], flat(bank[2], 2 * P), ACT.Copy, scale=inv[:, 0:1])
         nc.sync.dma_start(out_q[:, 0, 0 : 2 * P], y_early0[:])
-        y2 = keep.tile([P, QB, P], F32, name="y2")
+        y2 = keep.tile([P, QB, P], F32, name="y2", align_bytes=DMA_ALIGN)
         for b in range(QB):
             product(flat(bank[4 + b], P), b, codes2[:], scales2[:])
         nc.scalar.activation(y2[:, 0, :], flat(bank[4], P), ACT.Copy, scale=inv[:, 0:1])
@@ -228,7 +229,7 @@ def tile_attend_mqa_topk_ks_kernel(tc, qT, kT, vT, ks, vs, offs, out):
         quantize(codes3[:], scales3[:], last[:])
         nc.vector.tensor_scalar(y2[:, 1, :], flat(bank[5], P), inv[:, 1:2], None, MULT)
         nc.sync.dma_start(out_q[:, :, 2 * P : 3 * P], y2[:])
-        y3 = [keep.tile([P, P], F32, name=f"y3_{b}") for b in range(QB)]
+        y3 = [keep.tile([P, P], F32, name=f"y3_{b}", align_bytes=DMA_ALIGN) for b in range(QB)]
         product(flat(bank[6], P), 1, codes3[:], scales3[:])
         nc.vector.tensor_scalar(y3[1][:], flat(bank[6], P), inv[:, 1:2], None, MULT)
         nc.sync.dma_start(out_q[:, 1, 3 * P : 4 * P], y3[1][:])

@@ -180,7 +180,7 @@ def tile_attend_mqa_topk_ks_kernel(tc, qT, kT, vT, ks, vs, offs, out):
         early0 = keep.tile([P, 2 * P], F32, name="early0", tag="early0", align_bytes=64)
         early_scales = keep.tile([P, 2 * P], U8, name="early_scales", align_bytes=64)
         turn_values(0, bank[7])
-        nc.vector.tensor_copy(v_row[1][:], v_win[1][:].indirect(offsets[:]))
+        gather_shared(1, 128)
         weights(0, bank[5], "v_win1")
         weave(bank[7], early0[:])
         weights(1, bank[6], "w_bf1")

from contextlib import ExitStack

import concourse.mybir as mybir
from concourse.masks import make_identity

FLOPS = 2 * 2 * 256 * 512 * 512
BYTES = 4 * (512 * 256 + 2 * 512 * 2048 + 2 * 2048 + 256 * 512) + 2 * 128 * 32

F32 = mybir.dt.float32
BF16 = mybir.dt.bfloat16
U32 = mybir.dt.uint32
U16 = mybir.dt.uint16
U8 = mybir.dt.uint8
FP8X4 = mybir.dt.float8_e4m3fn_x4
MULT = mybir.AluOpType.mult
MIN = mybir.AluOpType.min
POW = mybir.AluOpType.pow
AXIS_X = mybir.AxisListType.X
ACT = mybir.ActivationFunctionType

P = 128
PACK = 4
T = 2048
N = 512
NQ = 256
DV = 512
QB = NQ // P
EB = DV // P
SB = N // P
DMA_ALIGN = 256


def tile_attend_mqa_topk_ks_kernel(tc, qT, kT, vT, ks, vs, offs, out):
    nc = tc.nc
    with ExitStack() as ctx:
        keep = ctx.enter_context(tc.tile_pool(name="keep", bufs=1))
        psum = ctx.enter_context(tc.psum_pool(name="psum", bufs=1))

        offsets = keep.tile([P, N // 16], U16, name="offsets")
        q_raw = keep.tile([P, PACK, NQ], F32, name="q_raw", align_bytes=DMA_ALIGN)
        k_win = [keep.tile([P, T], F32, name=f"k_win{t}", align_bytes=DMA_ALIGN) for t in range(PACK)]
        v_win = [keep.tile([P, T], F32, name=f"v_win{g}", tag=f"v_win{g}", align_bytes=DMA_ALIGN) for g in range(EB)]
        ks_win = keep.tile([P, T], F32, name="ks_win", align_bytes=DMA_ALIGN)
        vs_win = keep.tile([P, T], F32, name="vs_win", align_bytes=DMA_ALIGN)

        k_planes = kT.rearrange("(p j) n -> j p n", j=PACK)
        v_planes = vT.rearrange("(g e) n -> g e n", e=P)
        for t, (win, row) in enumerate(((ks_win, ks), (vs_win, vs))):
            nc.sync.dma_start(k_win[t][:], k_planes[t])
            if t == 0:
                nc.sync.dma_start(offsets[:], offs)
            nc.vector.memset(win[:], 0.0)
            nc.sync.dma_start(win[64 * t : 64 * t + 1, :], row[0:1, :])
        for t in (2, 3):
            nc.sync.dma_start(k_win[t][:], k_planes[t])
        nc.sync.dma_start(q_raw[:], qT[0].rearrange("(p j) q -> p j q", j=PACK))
        for g in range(EB):
            nc.sync.dma_start(v_win[g][:], v_planes[g])

        ident = keep.tile([P, P], F32, name="ident")
        make_identity(nc, ident[:])

        bank = [psum.tile([P, PACK, P], F32, name=f"bank{i}") for i in range(8)]

        def flat(tile, width):
            return tile[:].rearrange("p c s -> p (c s)")[:, 0:width]

        def by_place(row):
            return row.rearrange("p (s t) -> p t s", t=PACK)

        k_bf = keep.tile([P, N, PACK], BF16, name="k_bf", align_bytes=64)
        k_codes = keep.tile([P, N], U32, name="k_codes", align_bytes=64)
        k_scales = keep.tile([P, N], U8, name="k_scales", align_bytes=64)
        k_pair = keep.tile([P, 2, N], F32, name="k_pair")
        vs_row = keep.tile([P, N], F32, name="vs_row")
        ks_row = keep.tile([P, N], F32, name="ks_row")
        nks_col = keep.tile([P, SB], F32, name="nks_col")
        vs_col = keep.tile([P, PACK], F32, name="vs_col")
        nks_all = keep.tile([P, 2, PACK, N // 8], F32, name="nks_all")

        nc.scalar.activation(k_pair[:, 0, :], k_win[0][:].indirect(offsets[:]), ACT.Copy)
        nc.vector.tensor_copy(ks_row[:], ks_win[:].indirect(offsets[:]))
        nc.vector.tensor_copy(k_pair[:, 1, :], k_win[1][:].indirect(offsets[:]))
        nc.vector.tensor_copy(vs_row[:], vs_win[:].indirect(offsets[:]))
        for c in range(SB):
            nc.tensor.transpose(bank[2][:, c, :], ks_row[:, c * P : (c + 1) * P], ident[:])
        nc.scalar.activation(nks_col[:], bank[2][:, :, 0], ACT.Copy, scale=-1.0)
        for c in range(SB):
            nc.tensor.transpose(bank[3][:, c, :], nks_col[:, c : c + 1].to_broadcast([P, P]), ident[:])
        nc.scalar.copy(nks_all[:], flat(bank[3], N).rearrange("p (h s t) -> p h t s", h=2, t=PACK))
        nc.scalar.copy(k_bf[:, :, 0:2], k_pair[:].rearrange("p j n -> p n j"))
        for t in range(PACK):
            nc.tensor.transpose(bank[5][:, t, :], vs_row[:, t::PACK], ident[:])
        nc.scalar.copy(vs_col[:], bank[5][:, :, 64])
        nc.vector.tensor_copy(k_bf[:, :, 2], k_win[2][:].indirect(offsets[:]))
        halves = [slice(h * N // 2, (h + 1) * N // 2) for h in range(2)]
        lists = [offsets[:, h * N // 32 : (h + 1) * N // 32] for h in range(2)]
        for h, cols in enumerate(halves):
            nc.vector.tensor_copy(k_bf[:, cols, 3], k_win[3][:].indirect(lists[h]))

        q_bf = keep.tile([P, NQ, PACK], BF16, name="q_bf", align_bytes=64)
        q_codes = keep.tile([P, NQ], U32, name="q_codes", align_bytes=64)
        q_scales = keep.tile([P, NQ], U8, name="q_scales", tag="q_scales", align_bytes=64)
        for b, cols in enumerate(halves):
            rows = slice(b * P, (b + 1) * P)
            nc.vector.quantize_mx(
                k_codes[:, cols].bitcast(FP8X4), k_scales[:, cols], k_bf[:, cols, :].rearrange("p n j -> p (n j)")
            )
            nc.scalar.copy(
                q_bf[:, rows, :].rearrange("p (c i) j -> p c j i", i=4),
                q_raw[:, :, rows].rearrange("p j (c i) -> p c j i", i=4),
            )
            nc.vector.quantize_mx(
                q_codes[:, rows].bitcast(FP8X4), q_scales[:, rows], q_bf[:, rows, :].rearrange("p q j -> p (q j)")
            )

        neg_a = [keep.tile([P, 2, PACK, N // 8], F32, name=f"neg_a{b}") for b in range(QB)]
        for b in range(QB):
            rows = slice(b * P, (b + 1) * P)
            for h, cols in enumerate(halves):
                scores = flat(bank[2 * b + h], N // 2)
                nc.tensor.matmul_mx(
                    scores, q_codes[:, rows].bitcast(FP8X4), q_scales[:, rows],
                    k_codes[:, cols].bitcast(FP8X4), k_scales[:, cols], start=True, stop=True,
                )
                nc.vector.tensor_tensor(neg_a[b][:, h, :, :], by_place(scores), nks_all[:, h, :, :], MULT)

        v_row = [keep.tile([P, N], BF16, name=f"v_row{g}", tag=f"v_row{g}", align_bytes=DMA_ALIGN) for g in range(EB)]

        def gather_shared(g, scalar_slots):
            nc.scalar.activation(
                v_row[g][:, 0:scalar_slots], v_win[g][:].indirect(offsets[:, 0 : scalar_slots // 16]), ACT.Copy
            )
            nc.vector.tensor_copy(v_row[g][:, scalar_slots:], v_win[g][:].indirect(offsets[:, scalar_slots // 16 :]))

        def turn_values(g, turned):
            words = v_row[g][:].bitcast(F32)
            for u in range(2):
                nc.tensor.transpose(turned[:, u, :], words[:, u::2], ident[:])

        def weave(turned, dst):
            nc.scalar.copy(dst.rearrange("s (e u) -> s e u", u=2), turned[:, 0:2, :].rearrange("s u e -> s e u"))

        def quantize(codes, scales, words):
            nc.vector.quantize_mx(codes.bitcast(FP8X4), scales, words.bitcast(BF16))

        neg_m = [
            keep.tile([P, 1], F32, name="neg_m0", tag="q_scales", align_bytes=64),
            keep.tile([P, 1], F32, name="neg_m1", tag="early0", align_bytes=64),
        ]
        total = keep.tile([P, QB], F32, name="total")
        p_sb = [keep.tile([P, PACK, P], F32, name=f"p_sb{b}") for b in range(QB)]
        w_bf = []
        w_scales = [keep.tile([P, P], U8, name=f"w_scales{b}", align_bytes=64) for b in range(QB)]

        def weights(b, turned, tag):
            w_bf.append(keep.tile([P, P, PACK], BF16, name=f"w_bf{b}", tag=tag, align_bytes=DMA_ALIGN))
            for t in range(PACK):
                nc.tensor.transpose(turned[:, t, :], p_sb[b][:, t, :], ident[:])
            nc.vector.tensor_tensor(
                w_bf[b][:], turned[:].rearrange("s t q -> s q t"),
                vs_col[:].unsqueeze(1).to_broadcast([P, P, PACK]), MULT,
            )

        def quantize_w(b):
            nc.vector.quantize_mx(w_codes[b].bitcast(FP8X4), w_scales[b][:], w_bf[b][:].rearrange("s q t -> s (q t)"))

        nc.scalar.activation(v_row[0][:], v_win[0][:].indirect(offsets[:]), ACT.Copy)
        for b in range(QB):
            nc.vector.tensor_reduce(neg_m[b][:], neg_a[b][:].rearrange("p h t s -> p (h t s)"), AXIS_X, MIN)
            nc.scalar.activation(
                p_sb[b][:].rearrange("p t (h s) -> p h t s", h=2), neg_a[b][:], ACT.Exp,
                bias=neg_m[b][:], scale=-1.0, accum_out=total[:, b : b + 1],
            )
        minus_one = keep.tile([P, QB], F32, name="minus_one")
        nc.gpsimd.memset(minus_one[:], -1.0)
        inv = keep.tile([P, QB], F32, name="inv")
        nc.gpsimd.tensor_tensor(inv[:], total[:], minus_one[:], POW)

        early0 = keep.tile([P, 2 * P], F32, name="early0", tag="early0", align_bytes=64)
        early_scales = keep.tile([P, 2 * P], U8, name="early_scales", align_bytes=64)
        turn_values(0, bank[7])
        gather_shared(1, 128)
        weights(0, bank[5], "v_win1")
        weave(bank[7], early0[:])
        weights(1, bank[6], "w_bf1")
        turn_values(1, bank[0])
        early1 = keep.tile([P, 2 * P], F32, name="early1", align_bytes=64)
        weave(bank[0], early1[:])
        codes = keep.tile([P, 4 * P], U32, name="codes", align_bytes=64)
        early_codes = codes[:, 0 : 2 * P]
        w_codes = [codes[:, (2 + b) * P : (3 + b) * P] for b in range(QB)]
        quantize(early_codes[:, 0:P], early_scales[:, 0:P], early0[:])
        quantize_w(0)
        quantize_w(1)
        quantize(early_codes[:, P:], early_scales[:, P:], early1[:])
        gather_shared(2, 320)

        def product(y, b, v_codes, v_scales):
            nc.tensor.matmul_mx(
                y, w_codes[b].bitcast(FP8X4), w_scales[b][:], v_codes.bitcast(FP8X4), v_scales, start=True, stop=True
            )

        out_q = out[0].rearrange("(b q) e -> q b e", q=P)
        turn_values(2, bank[1])
        for b in range(QB):
            product(flat(bank[2 + b], 2 * P), b, early_codes, early_scales[:])

        gather_shared(3, 192)
        turn_values(3, bank[7])
        behind = keep.tile([P, 4 * P], F32, name="behind", tag="v_win3", align_bytes=DMA_ALIGN)
        weave(bank[1], behind[:, 0 : 2 * P])
        nc.vector.tensor_scalar(behind[:, 2 * P :], flat(bank[3], 2 * P), inv[:, 1:2], None, MULT)
        nc.sync.dma_start(out_q[:, 1, 0 : 2 * P], behind[:, 2 * P :])
        codes2 = keep.tile([P, P], U32, name="codes2", align_bytes=64)
        scales2 = keep.tile([P, P], U8, name="scales2", align_bytes=64)
        quantize(codes2[:], scales2[:], behind[:, 0 : 2 * P])
        last = keep.tile([P, 2 * P], F32, name="last", align_bytes=64)
        weave(bank[7], last[:])
        y_early0 = keep.tile([P, 2 * P], F32, name="y_early0", tag="v_row3", align_bytes=DMA_ALIGN)
        nc.scalar.activation(y_early0[:], flat(bank[2], 2 * P), ACT.Copy, scale=inv[:, 0:1])
        nc.sync.dma_start(out_q[:, 0, 0 : 2 * P], y_early0[:])
        y2 = keep.tile([P, QB, P], F32, name="y2", align_bytes=DMA_ALIGN)
        for b in range(QB):
            product(flat(bank[4 + b], P), b, codes2[:], scales2[:])
        nc.scalar.activation(y2[:, 0, :], flat(bank[4], P), ACT.Copy, scale=inv[:, 0:1])
        codes3 = keep.tile([P, P], U32, name="codes3", align_bytes=64)
        scales3 = keep.tile([P, P], U8, name="scales3", align_bytes=64)
        quantize(codes3[:], scales3[:], last[:])
        nc.vector.tensor_scalar(y2[:, 1, :], flat(bank[5], P), inv[:, 1:2], None, MULT)
        nc.sync.dma_start(out_q[:, :, 2 * P : 3 * P], y2[:])
        y3 = [keep.tile([P, P], F32, name=f"y3_{b}", align_bytes=DMA_ALIGN) for b in range(QB)]
        product(flat(bank[6], P), 1, codes3[:], scales3[:])
        nc.vector.tensor_scalar(y3[1][:], flat(bank[6], P), inv[:, 1:2], None, MULT)
        nc.sync.dma_start(out_q[:, 1, 3 * P : 4 * P], y3[1][:])
        product(flat(bank[0], P), 0, codes3[:], scales3[:])
        nc.scalar.activation(y3[0][:], flat(bank[0], P), ACT.Copy, scale=inv[:, 0:1])
        nc.scalar.dma_start(out_q[:, 0, 3 * P : 4 * P], y3[0][:])
